import numpy as np
import ml_dtypes


def mxq(x, axis, fmt="e4m3"):
    dtype, down = {"e4m3": (ml_dtypes.float8_e4m3fn, 7), "e5m2": (ml_dtypes.float8_e5m2, 14)}[fmt]
    v = np.moveaxis(np.asarray(x, np.float32).astype(ml_dtypes.bfloat16).astype(np.float64), axis, -1)
    blocks = v.reshape(v.shape[:-1] + (-1, 32))
    amax = np.abs(blocks).max(-1, keepdims=True)
    byte = np.maximum(np.where(amax > 0, np.frexp(amax)[1] - 1 + 127, 0) - down, 1)
    scale = np.exp2(byte - 127.0)
    codes = (blocks / scale).astype(np.float32).astype(dtype).astype(np.float64)
    return np.moveaxis((codes * scale).reshape(v.shape), -1, axis)


WIDE = False


def mx_kscale(k):
    if not WIDE:
        return np.ones(k)
    levels = np.array([10, -10, 5, -5, 0])
    if k % 512:
        return np.exp2(np.random.permutation(np.resize(levels, k // 32))).repeat(32)
    a = np.empty((k // 512, 16))
    for p in range(k // 512):
        a[p, :8] = np.random.permutation(np.resize(levels, 8))
        for g in range(8):
            far = levels[np.abs(levels - a[p, g]) >= 10]
            a[p, g + 8] = far[np.random.randint(len(far))]
    return np.exp2(a.ravel()).repeat(32)


def f64(x):
    return np.asarray(x).astype(np.float64)


def striped(idx):
    return np.tile(idx.reshape(-1, 16).T, (8, 1)).astype(np.uint16)


def unstriped(offs):
    return offs[:16].T.reshape(-1).astype(np.int64)


def striped8(idx):
    return np.concatenate([x.reshape(-1, 16).T for x in idx]).astype(np.uint16)


def runs(offs, k):
    lists = np.stack([offs[16 * r : 16 * r + 16].T.reshape(-1) for r in range(8)]).astype(np.int64)
    return lists[np.arange(k) % 512 // 64]


def pack_weight(w):
    k, n = w.shape
    w = f64(np.asarray(w, np.float32).astype(ml_dtypes.bfloat16)).reshape(k // 32, 32, n)
    amax = np.abs(w).max(1)
    byte = np.clip(np.where(amax > 0, np.frexp(amax)[1] - 1 + 127 - 7, 1), 1, 254)
    scaled = (w * np.exp2(127.0 - byte)[:, None, :]).reshape(k, n).astype(np.float32)
    words = np.ascontiguousarray(scaled.reshape(k // 512, 128, 4, n).transpose(0, 1, 3, 2)).astype(ml_dtypes.float8_e4m3fn).view(np.uint8)
    return words, np.ascontiguousarray(byte.astype(np.uint8).reshape(k // 512, 16, n))


def unpack_weight(words, scales):
    g, p, n, _ = words.shape
    vals = np.ascontiguousarray(words).view(ml_dtypes.float8_e4m3fn).astype(np.float64) * np.repeat(np.exp2(scales.astype(np.float64) - 127.0), 8, axis=1)[..., None]
    return vals.transpose(0, 1, 3, 2).reshape(g * 512, n)


def sigmoid(v):
    return 1.0 / (1.0 + np.exp(-np.maximum(v, -700.0)))

def planes(y):
    n, m = y.shape
    v = y.astype(np.float32).astype(ml_dtypes.bfloat16).astype(np.float64).reshape(n // 32, 32, m)
    top = np.abs(v).max(1)
    byte = np.clip(np.where(top > 0, np.frexp(top)[1] - 1 + 127 - 7, 1), 1, 254)
    codes = (v * np.exp2(127.0 - byte)[:, None, :]).reshape(n, m).astype(np.float32).astype(ml_dtypes.float8_e4m3fn).view(np.uint8)
    words = codes.reshape(n // 512, 128, 4, m).transpose(0, 1, 3, 2)
    return np.ascontiguousarray(words), np.ascontiguousarray(byte.astype(np.uint8).reshape(n // 512, 16, m))


K, T, S, N, H, W = 512, 2048, 512, 512, 512, 2048


def setup_inputs():
    n = np.random.standard_normal
    s = mx_kscale(K)[:, None]
    u = mx_kscale(S)
    packed_xT = pack_weight(n((K, T)) * s)
    packed_w1 = pack_weight(n((S, N)) / np.sqrt(S) / u[:, None])
    return {
        "x_words": packed_xT[0],
        "x_scales": packed_xT[1],
        "wa": (n((K, H)) / np.sqrt(K) / s).astype(np.float32),
        "wb": (n((K, H)) / np.sqrt(K) / s).astype(np.float32),
        "gt": (np.random.uniform(0.5, 1.5, (S, 1)) * u[:, None]).astype(np.float32),
        "w1_words": packed_w1[0],
        "w1_scales": packed_w1[1],
        "offs": striped(np.random.permutation(T)[:S]),
        "two": striped(np.random.permutation(T)[:S]),
        "n1": striped8(np.stack([np.random.permutation(H) for _ in range(8)])),
        "n2": striped8(np.stack([np.random.permutation(H) for _ in range(8)])),
        "n3": striped(np.random.randint(0, H, W)),
    }


def reference(x_words, x_scales, wa, wb, gt, w1_words, w1_scales, offs, two, n1, n2, n3):
    xq = unpack_weight(x_words, x_scales)[:, unstriped(offs)]
    y = xq.T @ mxq(f64(wa), 0, "e4m3")
    x_two = unpack_weight(x_words, x_scales)[:, unstriped(two)]
    d = x_two.T @ mxq(f64(wb), 0, "e4m3")
    z = f64(gt) * (y + (sigmoid(d[np.arange(S)[:, None], runs(n2, S)] - d)) * (y[np.arange(S)[:, None], runs(n1, S)] - y))
    h = unpack_weight(w1_words, w1_scales).T @ mxq(z, 0, "e4m3")
    ex = np.exp(0.5 * h)
    mb = ex[:, unstriped(n3)]
    ms = mb.reshape(N, H, 4).sum(axis=2)
    out_0 = (4.0 * ex) / (ms + 0.5)
    return (out_0,) + planes(out_0)

@@ -1,0 +1,317 @@
+from contextlib import ExitStack
+
+import concourse.mybir as mybir
+
+F32 = mybir.dt.float32
+BF16 = mybir.dt.bfloat16
+I32 = mybir.dt.int32
+U32 = mybir.dt.uint32
+U16 = mybir.dt.uint16
+U8 = mybir.dt.uint8
+FP8X4 = mybir.dt.float8_e4m3fn_x4
+ALU = mybir.AluOpType
+ACT = mybir.ActivationFunctionType
+
+K, T, S, N, H, W = 512, 2048, 512, 512, 512, 2048
+FLOPS = 2 * (2 * K * S * H + S * N * H)
+
+P = 128
+PACK = 4
+HALF = H // 2
+MEMBERS = W // H
+SPARE = 32
+MIX_CHUNKS = ((0, 256), (256, 384), (384, 512))
+OUT_CHUNKS = ((0, 64), (64, 128), (128, 192), (192, 320), (320, 448), (448, 512))
+SHIFT = 2.0 ** -120
+
+
+def tile_picked_twtpullbgshare_none_po_kernel(
+    tc, x_words, x_scales, wa, wb, gt, w1_words, w1_scales, offs, two, n1, n2, n3, out_0, out_1, out_2
+):
+    nc = tc.nc
+    with ExitStack() as ctx:
+        lists = ctx.enter_context(tc.tile_pool(name="lists", bufs=1))
+        sb = ctx.enter_context(tc.tile_pool(name="sb", bufs=1))
+        ps = ctx.enter_context(tc.psum_pool(name="ps", bufs=1))
+
+        def load_list(src, name):
+            tile = lists.tile(list(src.shape), U16, name=name)
+            nc.sync.dma_start(out=tile[:], in_=src)
+            return tile
+
+        def load_scale_rows(queue, tile, rows):
+            for q in range(4):
+                queue.dma_start(out=tile[32 * q : 32 * q + 4, :].bitcast(I32), in_=rows[4 * q : 4 * q + 4, :].bitcast(I32))
+
+        def dealt(ap):
+            return ap.rearrange("p (t m) -> p m t", t=PACK)
+
+        def load_half(w, h, name):
+            raw = sb.tile([P, PACK, HALF], F32, name=name)
+            nc.sync.dma_start(out=raw[:], in_=w.rearrange("(p j) n -> p j n", j=PACK)[:, :, h * HALF : (h + 1) * HALF])
+            return raw
+
+        def weave(dst, src):
+            return dst.rearrange("p (c i) t -> p c t i", i=4), src.rearrange("p t (c i) -> p c t i", i=4)
+
+        def quantize(codes, scales, grouped):
+            nc.vector.quantize_mx(out=codes.bitcast(FP8X4), scales=scales, in_=grouped.rearrange("p c t -> p (c t)"))
+
+        def product(out, lhs_words, lhs_scales, t, codes, scales):
+            rows = slice(t * P, (t + 1) * P)
+            nc.tensor.matmul_mx(
+                out=out, lhsT=lhs_words[:, rows].bitcast(FP8X4), lhsT_scale=lhs_scales[:, rows],
+                rhs=codes.bitcast(FP8X4), rhs_scale=scales, start=True, stop=True,
+            )
+
+        def fetch(out, window, offsets, first, last):
+            nc.scalar.activation(out=out, in_=window[:].indirect(offsets[:, first // 16 : last // 16]), func=ACT.Copy)
+
+        xs_win = sb.tile([P, T], U8, name="xs_win", align_bytes=64)
+        nc.vector.memset(xs_win[:, : T // 2].bitcast(I32), 0)
+        nc.gpsimd.memset(xs_win[:, T // 2 :].bitcast(I32), 0)
+        two_l = load_list(two, "two_l")
+        offs_l = load_list(offs, "offs_l")
+        n2_l = load_list(n2, "n2_l")
+        n1_l = load_list(n1, "n1_l")
+        xw_win = sb.tile([P, T], U32, name="xw_win", align_bytes=64)
+        nc.sync.dma_start(out=xw_win[:].bitcast(I32), in_=x_words[0].rearrange("p c r -> p (c r)").bitcast(I32))
+        load_scale_rows(nc.scalar, xs_win, x_scales[0])
+        wb_raw = [load_half(wb, h, f"wb_raw{h}") for h in range(2)]
+        n3_l = load_list(n3, "n3_l")
+        wa_raw = [load_half(wa, h, f"wa_raw{h}") for h in range(2)]
+        gate = sb.tile([P, PACK], F32, name="gate")
+        nc.sync.dma_start(out=gate[:], in_=gt.rearrange("(p t) one -> p (t one)", t=PACK))
+        w1w_raw = sb.tile([P, N], U32, name="w1w_raw", align_bytes=64)
+        nc.sync.dma_start(out=w1w_raw[:].bitcast(I32), in_=w1_words[0].rearrange("p c r -> p (c r)").bitcast(I32))
+        w1s_raw = sb.tile([P, N], U8, name="w1s_raw", align_bytes=64)
+        nc.gpsimd.memset(w1s_raw[:].bitcast(I32), 0)
+        load_scale_rows(nc.sync, w1s_raw, w1_scales[0])
+
+        half_gate = sb.tile([P, PACK], F32, name="half_gate")
+        nc.gpsimd.tensor_scalar(out=half_gate[:], in0=gate[:], scalar1=0.5, scalar2=0.0, op0=ALU.mult, op1=ALU.add)
+
+        ex = [sb.tile([P, H + SPARE], F32, name=f"ex{t}", align_bytes=64) for t in range(PACK)]
+        for t in range(PACK):
+            nc.gpsimd.memset(ex[t][:, H:], 0.0)
+
+        def pick(window, offsets, dtype, name):
+            tile = sb.tile([P, S], dtype, name=name, align_bytes=64)
+            nc.vector.tensor_copy(out=dealt(tile[:]), in_=window[:].indirect(offsets[:]))
+            return tile
+
+        xs_two = pick(xs_win, two_l, U8, "xs_two")
+        xs_off = pick(xs_win, offs_l, U8, "xs_off")
+        xw_two = pick(xw_win, two_l, U32, "xw_two")
+        xw_off = pick(xw_win, offs_l, U32, "xw_off")
+
+        def grouped_tile(name, cols):
+            return sb.tile([P, cols, PACK], BF16, name=name, tag=name, align_bytes=64)
+
+        def mx_tiles(name, cols):
+            return (sb.tile([P, cols], U32, name=name + "_codes", align_bytes=64),
+                    sb.tile([P, cols], U8, name=name + "_scales", align_bytes=64))
+
+        def round_scalar(dst, src):
+            o, i = weave(dst, src)
+            nc.scalar.copy(out=o, in_=i)
+
+        def round_vector(dst, src):
+            o, i = weave(dst, src)
+            nc.vector.tensor_copy(out=o, in_=i)
+
+        def round_gpsimd(dst, src):
+            nc.gpsimd.tensor_scalar(out=dst, in0=src.rearrange("p t c -> p c t"), scalar1=1.0, scalar2=0.0, op0=ALU.mult, op1=ALU.add)
+
+        wb_grp = [grouped_tile(f"wb_grp{h}", HALF) for h in range(2)]
+        wa_grp = [grouped_tile(f"wa_grp{h}", HALF) for h in range(2)]
+        wb_mx = [mx_tiles(f"wb{h}", HALF) for h in range(2)]
+        wa_mx = [mx_tiles(f"wa{h}", HALF) for h in range(2)]
+        d_ps = [ps.tile([P, H], F32, name=f"d_ps{t}", tag=f"bank{t}") for t in range(PACK)]
+        y_ps = [ps.tile([P, H], F32, name=f"y_ps{t}", tag=f"bank{PACK + t}") for t in range(PACK)]
+
+        round_scalar(wb_grp[0][:], wb_raw[0][:])
+        round_vector(wb_grp[1][:], wb_raw[1][:])
+        for h in range(2):
+            quantize(wb_mx[h][0][:], wb_mx[h][1][:], wb_grp[h][:])
+            for t in range(PACK):
+                product(d_ps[t][:, h * HALF : (h + 1) * HALF], xw_two, xs_two, t, wb_mx[h][0][:], wb_mx[h][1][:])
+        round_scalar(wa_grp[0][:], wa_raw[0][:])
+        round_gpsimd(wa_grp[1][:], wa_raw[1][:])
+
+        d_win = [sb.tile([P, H], F32, name=f"d_win{t}", align_bytes=64) for t in range(PACK)]
+        y_win = [sb.tile([P, H], F32, name=f"y_win{t}", align_bytes=64) for t in range(PACK)]
+        d_far = sb.tile([P, PACK, H], F32, name="d_far")
+        d_gap = sb.tile([P, PACK, H], F32, name="d_gap")
+        y_far = sb.tile([P, PACK, H], F32, name="y_far")
+        y_gap = sb.tile([P, PACK, H], F32, name="y_gap")
+        th = sb.tile([P, PACK, H], F32, name="th")
+        pull = sb.tile([P, PACK, H], F32, name="pull")
+
+        for t in range(PACK):
+            nc.vector.tensor_copy(out=d_win[t][:], in_=d_ps[t][:])
+            for h in range(2):
+                fetch(d_far[:, t, h * HALF : (h + 1) * HALF], d_win[t], n2_l, h * HALF, (h + 1) * HALF)
+            if t % 2 == 1:
+                h = t // 2
+                quantize(wa_mx[h][0][:], wa_mx[h][1][:], wa_grp[h][:])
+                for u in range(PACK):
+                    product(y_ps[u][:, h * HALF : (h + 1) * HALF], xw_off, xs_off, u, wa_mx[h][0][:], wa_mx[h][1][:])
+
+        for t in range(PACK):
+            nc.gpsimd.tensor_tensor(out=d_gap[:, t, :], in0=d_far[:, t, :], in1=d_win[t][:], op=ALU.subtract)
+        for t in range(PACK):
+            if t < 1:
+                nc.vector.tensor_scalar(out=y_win[t][:], in0=y_ps[t][:], scalar1=half_gate[:, t : t + 1], scalar2=None, op0=ALU.mult)
+            else:
+                nc.scalar.activation(out=y_win[t][:], in_=y_ps[t][:], func=ACT.Copy, scale=half_gate[:, t : t + 1])
+        w1w = sb.tile([P, N], U32, name="w1w", align_bytes=64)
+        w1s = sb.tile([P, N], U8, name="w1s", align_bytes=64)
+        nc.vector.tensor_copy(out=w1w[:].rearrange("p (t m) -> p t m", t=PACK), in_=w1w_raw[:].rearrange("p (m t) -> p t m", t=PACK))
+        nc.gpsimd.tensor_copy(out=w1s[:].rearrange("p (t m) -> p t m", t=PACK), in_=w1s_raw[:].rearrange("p (m t) -> p t m", t=PACK))
+
+        h_ps = [ps.tile([P, H], F32, name=f"h_ps{t}", tag=f"bank{t}") for t in range(PACK)]
+        z = [sb.tile([P, PACK, b - a], BF16, name=f"z{c}", align_bytes=64) for c, (a, b) in enumerate(MIX_CHUNKS)]
+
+        def mix_gap(c, t):
+            a, b = MIX_CHUNKS[c]
+            fetch(y_far[:, t, a:b], y_win[t], n1_l, a, b)
+            nc.vector.scalar_tensor_tensor(out=y_gap[:, t, a:b], in0=y_ps[t][:, a:b], scalar=half_gate[:, t : t + 1], in1=y_far[:, t, a:b], op0=ALU.mult, op1=ALU.subtract)
+
+        def mix_tanh(c, pair):
+            a, b = MIX_CHUNKS[c]
+            ts = slice(2 * pair, 2 * pair + 2)
+            nc.scalar.activation(out=th[:, ts, a:b], in_=d_gap[:, ts, a:b], func=ACT.Tanh, scale=0.5)
+
+        def mix_pull(c, pair):
+            a, b = MIX_CHUNKS[c]
+            ts = slice(2 * pair, 2 * pair + 2)
+            nc.vector.scalar_tensor_tensor(out=pull[:, ts, a:b], in0=th[:, ts, a:b], scalar=1.0, in1=y_gap[:, ts, a:b], op0=ALU.add, op1=ALU.mult)
+
+        def mix_out(c, t):
+            a, b = MIX_CHUNKS[c]
+            nc.vector.scalar_tensor_tensor(out=z[c][:, t, :], in0=y_ps[t][:, a:b], scalar=gate[:, t : t + 1], in1=pull[:, t, a:b], op0=ALU.mult, op1=ALU.subtract)
+
+        z_grp = [grouped_tile(f"z_grp{c}", b - a) for c, (a, b) in enumerate(MIX_CHUNKS)]
+
+        def mix_weave(c):
+            round_vector(z_grp[c][:], z[c][:])
+
+        def mix_product(c):
+            a, b = MIX_CHUNKS[c]
+            z_codes, z_scales = mx_tiles(f"z{c}", b - a)
+            quantize(z_codes[:], z_scales[:], z_grp[c][:])
+            for t in range(PACK):
+                product(h_ps[t][:, a:b], w1w, w1s, t, z_codes[:], z_scales[:])
+
+        last = len(MIX_CHUNKS) - 1
+        mix_tanh(0, 0)
+        mix_gap(0, 0)
+        mix_gap(0, 1)
+        for c in range(last + 1):
+            mix_tanh(c, 1)
+            mix_gap(c, 2)
+            mix_pull(c, 0)
+            mix_gap(c, 3)
+            if c > 0:
+                mix_weave(c - 1)
+            mix_out(c, 0)
+            mix_pull(c, 1)
+            mix_out(c, 1)
+            if c > 0:
+                mix_product(c - 1)
+            if c < last:
+                mix_tanh(c + 1, 0)
+                mix_gap(c + 1, 0)
+            mix_out(c, 2)
+            if c < last:
+                mix_gap(c + 1, 1)
+            mix_out(c, 3)
+        mix_weave(last)
+        mix_product(last)
+        for a, b in MIX_CHUNKS:
+            for t in range(PACK):
+                nc.scalar.activation(out=ex[t][:, a:b], in_=h_ps[t][:, a:b], func=ACT.Exp, scale=0.5)
+
+        out_rows = out_0.rearrange("(p t) j -> p t j", t=PACK)
+        out_words = out_1[0].rearrange("p c r -> p (c r)").bitcast(I32)
+        o_scales = sb.tile([P, H], U8, name="o_scales", align_bytes=64)
+        held = {}
+
+        def out_sums(c):
+            a, b = OUT_CHUNKS[c]
+            n = b - a
+            mb = sb.tile([P, PACK, n * MEMBERS], F32, name=f"mb{c}")
+            for t in range(PACK):
+                fetch(mb[:, t, :], ex[t], n3_l, a * MEMBERS, b * MEMBERS)
+            twos = sb.tile([P, PACK * n, 2], F32, name=f"twos{c}", tag="turn")
+            groups = mb[:].rearrange("p e (j m) -> p (e j) m", m=MEMBERS)
+            nc.vector.tensor_tensor(out=twos[:], in0=groups[:, :, 0:2], in1=groups[:, :, 2:4], op=ALU.add)
+            held[c, "twos"] = twos
+
+        def out_den(c):
+            a, b = OUT_CHUNKS[c]
+            den = sb.tile([P, 2, 2 * (b - a)], F32, name=f"den{c}")
+            twos = held[c, "twos"]
+            nc.vector.scalar_tensor_tensor(out=den[:].rearrange("p e j -> p (e j)"), in0=twos[:, :, 0], scalar=0.5, in1=twos[:, :, 1], op0=ALU.add, op1=ALU.add)
+            held[c, "den"] = den
+
+        def out_both(c):
+            a, b = OUT_CHUNKS[c]
+            both = sb.tile([P, 2 * (b - a)], F32, name=f"both{c}", tag="turn")
+            den = held[c, "den"]
+            nc.vector.scalar_tensor_tensor(out=both[:], in0=den[:, 0, :], scalar=SHIFT, in1=den[:, 1, :], op0=ALU.mult, op1=ALU.mult)
+            held[c, "both"] = both
+
+        def out_rec(c):
+            a, b = OUT_CHUNKS[c]
+            rec = sb.tile([P, 2 * (b - a)], F32, name=f"rec{c}")
+            nc.vector.reciprocal(out=rec[:], in_=held[c, "both"][:])
+            held[c, "rec"] = rec
+
+        def out_inv(c):
+            a, b = OUT_CHUNKS[c]
+            n = b - a
+            inv = sb.tile([P, 2, 2 * n], F32, name=f"inv{c}")
+            nc.vector.scalar_tensor_tensor(out=inv[:], in0=held[c, "den"][:], scalar=SHIFT, in1=held[c, "rec"][:].unsqueeze(1).to_broadcast([P, 2, 2 * n]), op0=ALU.mult, op1=ALU.mult)
+            held[c, "inv"] = inv[:].rearrange("p e (u j) -> p (e u) j", j=n)
+            held[c, "res"] = sb.tile([P, PACK, n], F32, name=f"res{c}")
+
+        def out_res(c, t):
+            a, b = OUT_CHUNKS[c]
+            nc.vector.scalar_tensor_tensor(out=held[c, "res"][:, t, :], in0=held[c, "inv"][:, (t + 2) % PACK, :], scalar=4.0, in1=ex[t][:, a:b], op0=ALU.mult, op1=ALU.mult)
+
+        def out_round(c):
+            a, b = OUT_CHUNKS[c]
+            nc.sync.dma_start(out=out_rows[:, :, a:b], in_=held[c, "res"][:])
+            held[c, "grp"] = grouped_tile(f"o_grp{c}", b - a)
+            round_vector(held[c, "grp"][:], held[c, "res"][:])
+
+        def out_planes(c):
+            a, b = OUT_CHUNKS[c]
+            o_codes = sb.tile([P, b - a], U32, name=f"o_codes{c}", align_bytes=64)
+            quantize(o_codes[:], o_scales[:, a:b], held[c, "grp"][:])
+            nc.sync.dma_start(out=out_words[:, a:b], in_=o_codes[:].bitcast(I32))
+
+        count = len(OUT_CHUNKS)
+        for c in range(count + 1):
+            now, old = c < count, c > 0
+            if now:
+                out_sums(c)
+            if old:
+                out_inv(c - 1)
+            if now:
+                out_den(c)
+            if old:
+                for t in range(PACK):
+                    out_res(c - 1, t)
+            if now:
+                out_both(c)
+            if old:
+                out_round(c - 1)
+            if now:
+                out_rec(c)
+            if old:
+                out_planes(c - 1)
+        for q in range(4):
+            nc.scalar.dma_start(out=out_2[0, 4 * q : 4 * q + 4, :].bitcast(I32), in_=o_scales[32 * q : 32 * q + 4, :].bitcast(I32))

@@ -1,6 +1,7 @@
 from contextlib import ExitStack
 
 import concourse.mybir as mybir
+from concourse.masks import make_identity
 
 F32 = mybir.dt.float32
 BF16 = mybir.dt.bfloat16
@@ -20,9 +21,7 @@ PACK = 4
 HALF = H // 2
 MEMBERS = W // H
 SPARE = 32
-MIX_CHUNKS = ((0, 256), (256, 384), (384, 512))
-OUT_CHUNKS = ((0, 64), (64, 128), (128, 192), (192, 320), (320, 448), (448, 512))
-SHIFT = 2.0 ** -120
+OUT_CHUNKS = ((0, 128), (128, 256), (256, 384), (384, 448), (448, 512))
 
 
 def tile_picked_twtpullbgshare_none_po_kernel(
@@ -64,24 +63,29 @@ def tile_picked_twtpullbgshare_none_po_kernel(
                 rhs=codes.bitcast(FP8X4), rhs_scale=scales, start=True, stop=True,
             )
 
-        def fetch(out, window, offsets, first, last):
-            nc.scalar.activation(out=out, in_=window[:].indirect(offsets[:, first // 16 : last // 16]), func=ACT.Copy)
+        def fetch(out, window, offsets, first, last, scale=1.0, bias=0.0):
+            nc.scalar.activation(out=out, in_=window[:].indirect(offsets[:, first // 16 : last // 16]), func=ACT.Copy, scale=scale, bias=bias)
+
+        def pieces(a, b):
+            return [(s, min(s + HALF, b)) for s in range(a, b, HALF)]
 
         xs_win = sb.tile([P, T], U8, name="xs_win", align_bytes=64)
-        nc.vector.memset(xs_win[:, : T // 2].bitcast(I32), 0)
-        nc.gpsimd.memset(xs_win[:, T // 2 :].bitcast(I32), 0)
+        nc.vector.memset(xs_win[:].bitcast(I32), 0)
         two_l = load_list(two, "two_l")
         offs_l = load_list(offs, "offs_l")
+        gate = sb.tile([P, PACK], F32, name="gate")
+        nc.sync.dma_start(out=gate[:], in_=gt.rearrange("(p t) one -> p (t one)", t=PACK))
         n2_l = load_list(n2, "n2_l")
         n1_l = load_list(n1, "n1_l")
         xw_win = sb.tile([P, T], U32, name="xw_win", align_bytes=64)
-        nc.sync.dma_start(out=xw_win[:].bitcast(I32), in_=x_words[0].rearrange("p c r -> p (c r)").bitcast(I32))
-        load_scale_rows(nc.scalar, xs_win, x_scales[0])
-        wb_raw = [load_half(wb, h, f"wb_raw{h}") for h in range(2)]
+        x_rows = x_words[0].rearrange("p c r -> p (c r)").bitcast(I32)
+        for h in range(2):
+            cols = slice(h * T // 2, (h + 1) * T // 2)
+            nc.sync.dma_start(out=xw_win[:, cols].bitcast(I32), in_=x_rows[:, cols])
         n3_l = load_list(n3, "n3_l")
+        load_scale_rows(nc.sync, xs_win, x_scales[0])
+        wb_raw = [load_half(wb, h, f"wb_raw{h}") for h in range(2)]
         wa_raw = [load_half(wa, h, f"wa_raw{h}") for h in range(2)]
-        gate = sb.tile([P, PACK], F32, name="gate")
-        nc.sync.dma_start(out=gate[:], in_=gt.rearrange("(p t) one -> p (t one)", t=PACK))
         w1w_raw = sb.tile([P, N], U32, name="w1w_raw", align_bytes=64)
         nc.sync.dma_start(out=w1w_raw[:].bitcast(I32), in_=w1_words[0].rearrange("p c r -> p (c r)").bitcast(I32))
         w1s_raw = sb.tile([P, N], U8, name="w1s_raw", align_bytes=64)
@@ -89,21 +93,24 @@ def tile_picked_twtpullbgshare_none_po_kernel(
         load_scale_rows(nc.sync, w1s_raw, w1_scales[0])
 
         half_gate = sb.tile([P, PACK], F32, name="half_gate")
-        nc.gpsimd.tensor_scalar(out=half_gate[:], in0=gate[:], scalar1=0.5, scalar2=0.0, op0=ALU.mult, op1=ALU.add)
+        nc.vector.tensor_scalar(out=half_gate[:], in0=gate[:], scalar1=0.5, scalar2=None, op0=ALU.mult)
 
         ex = [sb.tile([P, H + SPARE], F32, name=f"ex{t}", align_bytes=64) for t in range(PACK)]
         for t in range(PACK):
             nc.gpsimd.memset(ex[t][:, H:], 0.0)
+        d_win = [sb.tile([P, 2 * H], F32, name=f"d_win{t}", align_bytes=64) for t in range(PACK)]
+        for t in range(PACK):
+            nc.gpsimd.memset(d_win[t][:, H:], 0.0)
+        ident = sb.tile([P, P], F32, name="ident")
+        make_identity(nc, ident[:])
 
-        def pick(window, offsets, dtype, name):
-            tile = sb.tile([P, S], dtype, name=name, align_bytes=64)
+        def pick(window, offsets, dtype, name, tag=""):
+            tile = sb.tile([P, S], dtype, name=name, tag=tag or name, align_bytes=64)
             nc.vector.tensor_copy(out=dealt(tile[:]), in_=window[:].indirect(offsets[:]))
             return tile
 
-        xs_two = pick(xs_win, two_l, U8, "xs_two")
-        xs_off = pick(xs_win, offs_l, U8, "xs_off")
         xw_two = pick(xw_win, two_l, U32, "xw_two")
-        xw_off = pick(xw_win, offs_l, U32, "xw_off")
+        xs_two = pick(xs_win, two_l, U8, "xs_two")
 
         def grouped_tile(name, cols):
             return sb.tile([P, cols, PACK], BF16, name=name, tag=name, align_bytes=64)
@@ -123,195 +130,211 @@ def tile_picked_twtpullbgshare_none_po_kernel(
         def round_gpsimd(dst, src):
             nc.gpsimd.tensor_scalar(out=dst, in0=src.rearrange("p t c -> p c t"), scalar1=1.0, scalar2=0.0, op0=ALU.mult, op1=ALU.add)
 
-        wb_grp = [grouped_tile(f"wb_grp{h}", HALF) for h in range(2)]
-        wa_grp = [grouped_tile(f"wa_grp{h}", HALF) for h in range(2)]
-        wb_mx = [mx_tiles(f"wb{h}", HALF) for h in range(2)]
-        wa_mx = [mx_tiles(f"wa{h}", HALF) for h in range(2)]
+        wb_grp, wa_grp = grouped_tile("wb_grp", H), grouped_tile("wa_grp", H)
+        wb_codes, wb_scales = mx_tiles("wb", H)
+        wa_codes, wa_scales = mx_tiles("wa", H)
         d_ps = [ps.tile([P, H], F32, name=f"d_ps{t}", tag=f"bank{t}") for t in range(PACK)]
         y_ps = [ps.tile([P, H], F32, name=f"y_ps{t}", tag=f"bank{PACK + t}") for t in range(PACK)]
 
-        round_scalar(wb_grp[0][:], wb_raw[0][:])
-        round_vector(wb_grp[1][:], wb_raw[1][:])
-        for h in range(2):
-            quantize(wb_mx[h][0][:], wb_mx[h][1][:], wb_grp[h][:])
+        round_scalar(wb_grp[:, :HALF], wb_raw[0][:])
+        round_vector(wb_grp[:, HALF:], wb_raw[1][:])
+        quantize(wb_codes[:], wb_scales[:], wb_grp[:])
+        for t in range(PACK):
+            product(d_ps[t][:], xw_two, xs_two, t, wb_codes[:], wb_scales[:])
+        xw_off = pick(xw_win, offs_l, U32, "xw_off", tag="wb_grp")
+        xs_off = pick(xs_win, offs_l, U8, "xs_off", tag="xs_two")
+        round_gpsimd(wa_grp[:, :HALF], wa_raw[0][:])
+        round_vector(wa_grp[:, HALF:], wa_raw[1][:])
+
+        def y_products():
+            quantize(wa_codes[:], wa_scales[:], wa_grp[:])
             for t in range(PACK):
-                product(d_ps[t][:, h * HALF : (h + 1) * HALF], xw_two, xs_two, t, wb_mx[h][0][:], wb_mx[h][1][:])
-        round_scalar(wa_grp[0][:], wa_raw[0][:])
-        round_gpsimd(wa_grp[1][:], wa_raw[1][:])
+                product(y_ps[t][:], xw_off, xs_off, t, wa_codes[:], wa_scales[:])
 
-        d_win = [sb.tile([P, H], F32, name=f"d_win{t}", align_bytes=64) for t in range(PACK)]
-        y_win = [sb.tile([P, H], F32, name=f"y_win{t}", align_bytes=64) for t in range(PACK)]
-        d_far = sb.tile([P, PACK, H], F32, name="d_far")
-        d_gap = sb.tile([P, PACK, H], F32, name="d_gap")
-        y_far = sb.tile([P, PACK, H], F32, name="y_far")
-        y_gap = sb.tile([P, PACK, H], F32, name="y_gap")
-        th = sb.tile([P, PACK, H], F32, name="th")
-        pull = sb.tile([P, PACK, H], F32, name="pull")
+        z = sb.tile([P, 2, PACK, HALF], BF16, name="z", align_bytes=64)
+        y_win, y_far, d_gap, th = {}, {}, {}, {}
 
-        for t in range(PACK):
-            nc.vector.tensor_copy(out=d_win[t][:], in_=d_ps[t][:])
-            for h in range(2):
-                fetch(d_far[:, t, h * HALF : (h + 1) * HALF], d_win[t], n2_l, h * HALF, (h + 1) * HALF)
-            if t % 2 == 1:
-                h = t // 2
-                quantize(wa_mx[h][0][:], wa_mx[h][1][:], wa_grp[h][:])
-                for u in range(PACK):
-                    product(y_ps[u][:, h * HALF : (h + 1) * HALF], xw_off, xs_off, u, wa_mx[h][0][:], wa_mx[h][1][:])
+        def row_tile(name, tag=""):
+            return sb.tile([P, H], F32, name=name, tag=tag or name, align_bytes=64)
 
-        for t in range(PACK):
-            nc.gpsimd.tensor_tensor(out=d_gap[:, t, :], in0=d_far[:, t, :], in1=d_win[t][:], op=ALU.subtract)
-        for t in range(PACK):
-            if t < 1:
-                nc.vector.tensor_scalar(out=y_win[t][:], in0=y_ps[t][:], scalar1=half_gate[:, t : t + 1], scalar2=None, op0=ALU.mult)
+        def d_rows(t, tag=""):
+            if t < 2:
+                nc.scalar.copy(out=d_win[t][:, :H], in_=d_ps[t][:])
             else:
-                nc.scalar.activation(out=y_win[t][:], in_=y_ps[t][:], func=ACT.Copy, scale=half_gate[:, t : t + 1])
-        w1w = sb.tile([P, N], U32, name="w1w", align_bytes=64)
-        w1s = sb.tile([P, N], U8, name="w1s", align_bytes=64)
-        nc.vector.tensor_copy(out=w1w[:].rearrange("p (t m) -> p t m", t=PACK), in_=w1w_raw[:].rearrange("p (m t) -> p t m", t=PACK))
-        nc.gpsimd.tensor_copy(out=w1s[:].rearrange("p (t m) -> p t m", t=PACK), in_=w1s_raw[:].rearrange("p (m t) -> p t m", t=PACK))
+                nc.vector.tensor_copy(out=d_win[t][:, :H], in_=d_ps[t][:])
+            d_far = row_tile(f"d_far{t}", tag)
+            fetch(d_far[:], d_win[t], n2_l, 0, H)
+            d_gap[t] = row_tile(f"d_gap{t}")
+            nc.gpsimd.tensor_tensor(out=d_gap[t][:], in0=d_far[:], in1=d_win[t][:, :H], op=ALU.subtract)
 
-        h_ps = [ps.tile([P, H], F32, name=f"h_ps{t}", tag=f"bank{t}") for t in range(PACK)]
-        z = [sb.tile([P, PACK, b - a], BF16, name=f"z{c}", align_bytes=64) for c, (a, b) in enumerate(MIX_CHUNKS)]
+        def th_rows(t, tag=""):
+            th[t] = row_tile(f"th{t}", tag)
+            nc.scalar.activation(out=th[t][:], in_=d_gap[t][:], func=ACT.Tanh, scale=0.5)
 
-        def mix_gap(c, t):
-            a, b = MIX_CHUNKS[c]
-            fetch(y_far[:, t, a:b], y_win[t], n1_l, a, b)
-            nc.vector.scalar_tensor_tensor(out=y_gap[:, t, a:b], in0=y_ps[t][:, a:b], scalar=half_gate[:, t : t + 1], in1=y_far[:, t, a:b], op0=ALU.mult, op1=ALU.subtract)
+        def y_rows(t, tag=""):
+            y_win[t] = row_tile(f"y_win{t}")
+            nc.vector.tensor_scalar(out=y_win[t][:], in0=y_ps[t][:], scalar1=half_gate[:, t : t + 1], scalar2=None, op0=ALU.mult)
+            y_far[t] = row_tile(f"y_far{t}", tag)
+            for s, e in pieces(0, H):
+                fetch(y_far[t][:, s:e], y_win[t], n1_l, s, e)
 
-        def mix_tanh(c, pair):
-            a, b = MIX_CHUNKS[c]
-            ts = slice(2 * pair, 2 * pair + 2)
-            nc.scalar.activation(out=th[:, ts, a:b], in_=d_gap[:, ts, a:b], func=ACT.Tanh, scale=0.5)
+        def halves(ap):
+            return ap.rearrange("p (h c) -> p h c", c=HALF)
 
-        def mix_pull(c, pair):
-            a, b = MIX_CHUNKS[c]
-            ts = slice(2 * pair, 2 * pair + 2)
-            nc.vector.scalar_tensor_tensor(out=pull[:, ts, a:b], in0=th[:, ts, a:b], scalar=1.0, in1=y_gap[:, ts, a:b], op0=ALU.add, op1=ALU.mult)
+        def mix(step, t, a, b, early=None):
+            if early is None:
+                y_gap = sb.tile([P, b - a], F32, name=f"y_gap{step}", tag=f"mix{step % 2}")
+                nc.vector.scalar_tensor_tensor(out=y_gap[:], in0=y_ps[t][:, a:b], scalar=half_gate[:, t : t + 1], in1=y_far[t][:, a:b], op0=ALU.mult, op1=ALU.subtract)
+            else:
+                y_gap = early
+            pull = sb.tile([P, b - a], F32, name=f"pull{t}_{a}", tag=f"mix{(step + 1) % 2}")
+            nc.vector.scalar_tensor_tensor(out=pull[:], in0=th[t][:, a:b], scalar=1.0, in1=y_gap[:], op0=ALU.add, op1=ALU.mult)
+            nc.vector.scalar_tensor_tensor(out=z[:, a // HALF : b // HALF, t, :], in0=halves(y_ps[t][:, a:b]), scalar=gate[:, t : t + 1], in1=halves(pull[:]), op0=ALU.mult, op1=ALU.subtract)
 
-        def mix_out(c, t):
-            a, b = MIX_CHUNKS[c]
-            nc.vector.scalar_tensor_tensor(out=z[c][:, t, :], in0=y_ps[t][:, a:b], scalar=gate[:, t : t + 1], in1=pull[:, t, a:b], op0=ALU.mult, op1=ALU.subtract)
+        def deal_w1():
+            nc.gpsimd.tensor_copy(out=w1w[:].rearrange("p (t m) -> p t m", t=PACK), in_=w1w_raw[:].rearrange("p (m t) -> p t m", t=PACK))
+            nc.gpsimd.tensor_copy(out=w1s[:].rearrange("p (t m) -> p t m", t=PACK), in_=w1s_raw[:].rearrange("p (m t) -> p t m", t=PACK))
 
-        z_grp = [grouped_tile(f"z_grp{c}", b - a) for c, (a, b) in enumerate(MIX_CHUNKS)]
+        d_rows(0)
+        d_rows(1)
+        y_products()
+        th_rows(0)
+        y_rows(0)
+        d_rows(2)
+        y_rows(1, "d_gap0")
+        th_rows(1, "y_win0")
+        d_rows(3, "y_win1")
+        w1w = sb.tile([P, N], U32, name="w1w", tag="wa_grp", align_bytes=64)
+        w1s = sb.tile([P, N], U8, name="w1s", tag="d_far1", align_bytes=64)
+        deal_w1()
+        mix(0, 0, 0, H)
+        y_rows(2, "d_gap1")
+        th_rows(2, "y_win2")
+        mix(1, 1, 0, H)
+        th_rows(3)
+        y_rows(3, "d_gap2")
+        mix(2, 2, 0, H)
+        z_grp = [grouped_tile(f"z_grp{h}", HALF) for h in range(2)]
+        z_mx = [mx_tiles(f"z{h}", HALF) for h in range(2)]
+        h_ps = [[ps.tile([P, HALF], F32, name=f"h_ps{h}_{t}", tag=f"bank{PACK * h + t}") for t in range(PACK)] for h in range(2)]
 
-        def mix_weave(c):
-            round_vector(z_grp[c][:], z[c][:])
-
-        def mix_product(c):
-            a, b = MIX_CHUNKS[c]
-            z_codes, z_scales = mx_tiles(f"z{c}", b - a)
-            quantize(z_codes[:], z_scales[:], z_grp[c][:])
+        def places(h):
+            round_vector(z_grp[h][:], z[:, h])
+            quantize(z_mx[h][0][:], z_mx[h][1][:], z_grp[h][:])
             for t in range(PACK):
-                product(h_ps[t][:, a:b], w1w, w1s, t, z_codes[:], z_scales[:])
+                product(h_ps[h][t][:], w1w, w1s, t, z_mx[h][0][:], z_mx[h][1][:])
 
-        last = len(MIX_CHUNKS) - 1
-        mix_tanh(0, 0)
-        mix_gap(0, 0)
-        mix_gap(0, 1)
-        for c in range(last + 1):
-            mix_tanh(c, 1)
-            mix_gap(c, 2)
-            mix_pull(c, 0)
-            mix_gap(c, 3)
-            if c > 0:
-                mix_weave(c - 1)
-            mix_out(c, 0)
-            mix_pull(c, 1)
-            mix_out(c, 1)
-            if c > 0:
-                mix_product(c - 1)
-            if c < last:
-                mix_tanh(c + 1, 0)
-                mix_gap(c + 1, 0)
-            mix_out(c, 2)
-            if c < last:
-                mix_gap(c + 1, 1)
-            mix_out(c, 3)
-        mix_weave(last)
-        mix_product(last)
-        for a, b in MIX_CHUNKS:
-            for t in range(PACK):
-                nc.scalar.activation(out=ex[t][:, a:b], in_=h_ps[t][:, a:b], func=ACT.Exp, scale=0.5)
+        def exp_rows(t, h):
+            nc.scalar.activation(out=ex[t][:, h * HALF : (h + 1) * HALF], in_=h_ps[h][t][:], func=ACT.Exp, scale=0.5)
+
+        late_gap = sb.tile([P, H], F32, name="late_gap")
+        for s, e in pieces(0, H):
+            nc.gpsimd.tensor_tensor(out=late_gap[:, s:e], in0=y_win[3][:, s:e], in1=y_far[3][:, s:e], op=ALU.subtract)
+        mix(2, 3, 0, HALF, early=late_gap[:, :HALF])
+        places(0)
+        for t in range(PACK):
+            exp_rows(t, 0)
+        mix(2, 3, HALF, H, early=late_gap[:, HALF:])
+        places(1)
 
         out_rows = out_0.rearrange("(p t) j -> p t j", t=PACK)
         out_words = out_1[0].rearrange("p c r -> p (c r)").bitcast(I32)
         o_scales = sb.tile([P, H], U8, name="o_scales", align_bytes=64)
+        res = [sb.tile([P, PACK, b - a], F32, name=f"res{c}") for c, (a, b) in enumerate(OUT_CHUNKS)]
+        last = len(OUT_CHUNKS) - 1
+        blocks = []
+        for c, (a, b) in enumerate(OUT_CHUNKS):
+            rows = P // (b - a)
+            for first in range(0, PACK, rows):
+                blocks.append((c, first, rows))
+        turned = blocks[:-1]
         held = {}
 
-        def out_sums(c):
+        def members(c, first, rows):
             a, b = OUT_CHUNKS[c]
-            n = b - a
-            mb = sb.tile([P, PACK, n * MEMBERS], F32, name=f"mb{c}")
-            for t in range(PACK):
-                fetch(mb[:, t, :], ex[t], n3_l, a * MEMBERS, b * MEMBERS)
-            twos = sb.tile([P, PACK * n, 2], F32, name=f"twos{c}", tag="turn")
-            groups = mb[:].rearrange("p e (j m) -> p (e j) m", m=MEMBERS)
-            nc.vector.tensor_tensor(out=twos[:], in0=groups[:, :, 0:2], in1=groups[:, :, 2:4], op=ALU.add)
-            held[c, "twos"] = twos
+            mb = sb.tile([P, rows, (b - a) * MEMBERS], F32, name=f"mb{c}_{first}", tag="mb", bufs=3)
+            for e in range(rows):
+                fetch(mb[:, e, :], ex[first + e], n3_l, a * MEMBERS, b * MEMBERS, scale=0.25, bias=0.03125)
+            return mb[:].rearrange("p e (j m) -> p (e j) m", m=MEMBERS)
 
-        def out_den(c):
-            a, b = OUT_CHUNKS[c]
-            den = sb.tile([P, 2, 2 * (b - a)], F32, name=f"den{c}")
-            twos = held[c, "twos"]
-            nc.vector.scalar_tensor_tensor(out=den[:].rearrange("p e j -> p (e j)"), in0=twos[:, :, 0], scalar=0.5, in1=twos[:, :, 1], op0=ALU.add, op1=ALU.add)
-            held[c, "den"] = den
+        def turned_sums(k):
+            mb = members(*turned[k])
+            den = ps.tile([P, P], F32, name=f"den{k}", tag=f"bank{PACK + k % 3}")
+            for m in range(MEMBERS):
+                nc.tensor.matmul(den[:], lhsT=mb[:, :, m], rhs=ident[:], is_transpose=True, start=(m == 0), stop=(m == MEMBERS - 1))
+            held[k, "den"] = den
 
-        def out_both(c):
-            a, b = OUT_CHUNKS[c]
-            both = sb.tile([P, 2 * (b - a)], F32, name=f"both{c}", tag="turn")
-            den = held[c, "den"]
-            nc.vector.scalar_tensor_tensor(out=both[:], in0=den[:, 0, :], scalar=SHIFT, in1=den[:, 1, :], op0=ALU.mult, op1=ALU.mult)
-            held[c, "both"] = both
+        def turned_rec(k):
+            rec = sb.tile([P, P], F32, name=f"rec{k}")
+            nc.vector.reciprocal(out=rec[:], in_=held[k, "den"][:])
+            held[k, "rec"] = rec
 
-        def out_rec(c):
-            a, b = OUT_CHUNKS[c]
-            rec = sb.tile([P, 2 * (b - a)], F32, name=f"rec{c}")
-            nc.vector.reciprocal(out=rec[:], in_=held[c, "both"][:])
-            held[c, "rec"] = rec
+        def turned_back(k):
+            back = ps.tile([P, P], F32, name=f"back{k}", tag=f"bank{k % PACK}")
+            nc.tensor.transpose(back[:], held[k, "rec"][:], ident[:])
+            held[k, "back"] = back
 
-        def out_inv(c):
+        def turned_res(k):
+            c, first, rows = turned[k]
             a, b = OUT_CHUNKS[c]
-            n = b - a
-            inv = sb.tile([P, 2, 2 * n], F32, name=f"inv{c}")
-            nc.vector.scalar_tensor_tensor(out=inv[:], in0=held[c, "den"][:], scalar=SHIFT, in1=held[c, "rec"][:].unsqueeze(1).to_broadcast([P, 2, 2 * n]), op0=ALU.mult, op1=ALU.mult)
-            held[c, "inv"] = inv[:].rearrange("p e (u j) -> p (e u) j", j=n)
-            held[c, "res"] = sb.tile([P, PACK, n], F32, name=f"res{c}")
+            for e in range(rows):
+                t = first + e
+                nc.vector.tensor_tensor(out=res[c][:, t, :], in0=held[k, "back"][:, e * (b - a) : (e + 1) * (b - a)], in1=ex[t][:, a:b], op=ALU.mult)
+            if first + rows == PACK:
+                planes(c, round_vector)
 
-        def out_res(c, t):
+        def planes(c, rounding):
             a, b = OUT_CHUNKS[c]
-            nc.vector.scalar_tensor_tensor(out=held[c, "res"][:, t, :], in0=held[c, "inv"][:, (t + 2) % PACK, :], scalar=4.0, in1=ex[t][:, a:b], op0=ALU.mult, op1=ALU.mult)
-
-        def out_round(c):
-            a, b = OUT_CHUNKS[c]
-            nc.sync.dma_start(out=out_rows[:, :, a:b], in_=held[c, "res"][:])
-            held[c, "grp"] = grouped_tile(f"o_grp{c}", b - a)
-            round_vector(held[c, "grp"][:], held[c, "res"][:])
-
-        def out_planes(c):
-            a, b = OUT_CHUNKS[c]
+            nc.sync.dma_start(out=out_rows[:, :, a:b], in_=res[c][:])
+            o_grp = grouped_tile(f"o_grp{c}", b - a)
+            rounding(o_grp[:], res[c][:])
             o_codes = sb.tile([P, b - a], U32, name=f"o_codes{c}", align_bytes=64)
-            quantize(o_codes[:], o_scales[:, a:b], held[c, "grp"][:])
+            quantize(o_codes[:], o_scales[:, a:b], o_grp[:])
             nc.sync.dma_start(out=out_words[:, a:b], in_=o_codes[:].bitcast(I32))
 
-        count = len(OUT_CHUNKS)
-        for c in range(count + 1):
-            now, old = c < count, c > 0
-            if now:
-                out_sums(c)
-            if old:
-                out_inv(c - 1)
-            if now:
-                out_den(c)
-            if old:
-                for t in range(PACK):
-                    out_res(c - 1, t)
-            if now:
-                out_both(c)
-            if old:
-                out_round(c - 1)
-            if now:
-                out_rec(c)
-            if old:
-                out_planes(c - 1)
+        def straight_sums(t):
+            a, b = OUT_CHUNKS[last]
+            mb = members(last, t, 1)
+            twos = sb.tile([P, b - a, 2], F32, name=f"twos{t}")
+            nc.vector.tensor_tensor(out=twos[:], in0=mb[:, :, 0:2], in1=mb[:, :, 2:4], op=ALU.add)
+            held[t, "twos"] = twos
+
+        def straight_den(t):
+            a, b = OUT_CHUNKS[last]
+            den = sb.tile([P, b - a], F32, name=f"straight_den{t}")
+            nc.vector.tensor_tensor(out=den[:], in0=held[t, "twos"][:, :, 0], in1=held[t, "twos"][:, :, 1], op=ALU.add)
+            held[t, "straight_den"] = den
+
+        def straight_rec(t):
+            a, b = OUT_CHUNKS[last]
+            rec = sb.tile([P, b - a], F32, name=f"straight_rec{t}")
+            nc.vector.reciprocal(out=rec[:], in_=held[t, "straight_den"][:])
+            held[t, "straight_rec"] = rec
+
+        def straight_res(t):
+            a, b = OUT_CHUNKS[last]
+            nc.vector.tensor_tensor(out=res[last][:, t, :], in0=held[t, "straight_rec"][:], in1=ex[t][:, a:b], op=ALU.mult)
+
+        for k in range(len(turned)):
+            if k < PACK:
+                exp_rows(k, 1)
+            turned_sums(k)
+            if k > 0:
+                turned_back(k - 1)
+            turned_rec(k)
+            if k > 0:
+                turned_res(k - 1)
+        end = len(turned) - 1
+        turned_back(end)
+        straight_sums(2)
+        straight_sums(3)
+        straight_den(2)
+        straight_den(3)
+        straight_rec(2)
+        turned_res(end)
+        straight_rec(3)
+        straight_res(2)
+        straight_res(3)
+        planes(last, round_vector)
         for q in range(4):
             nc.scalar.dma_start(out=out_2[0, 4 * q : 4 * q + 4, :].bitcast(I32), in_=o_scales[32 * q : 32 * q + 4, :].bitcast(I32))

@@ -21,7 +21,9 @@ PACK = 4
 HALF = H // 2
 MEMBERS = W // H
 SPARE = 32
-OUT_CHUNKS = ((0, 128), (128, 256), (256, 384), (384, 448), (448, 512))
+WB_LOADS = ((0, 256), (256, 384), (384, 512))
+OUT_CHUNKS = ((0, 128), (128, 256), (256, 384), (384, 512))
+TURNED = 4
 
 
 def tile_picked_twtpullbgshare_none_po_kernel(
@@ -45,9 +47,9 @@ def tile_picked_twtpullbgshare_none_po_kernel(
         def dealt(ap):
             return ap.rearrange("p (t m) -> p m t", t=PACK)
 
-        def load_half(w, h, name):
-            raw = sb.tile([P, PACK, HALF], F32, name=name)
-            nc.sync.dma_start(out=raw[:], in_=w.rearrange("(p j) n -> p j n", j=PACK)[:, :, h * HALF : (h + 1) * HALF])
+        def load_columns(w, a, b, name):
+            raw = sb.tile([P, PACK, b - a], F32, name=name, align_bytes=64)
+            nc.sync.dma_start(out=raw[:], in_=w.rearrange("(p j) n -> p j n", j=PACK)[:, :, a:b])
             return raw
 
         def weave(dst, src):
@@ -77,15 +79,13 @@ def tile_picked_twtpullbgshare_none_po_kernel(
         nc.sync.dma_start(out=gate[:], in_=gt.rearrange("(p t) one -> p (t one)", t=PACK))
         n2_l = load_list(n2, "n2_l")
         n1_l = load_list(n1, "n1_l")
-        xw_win = sb.tile([P, T], U32, name="xw_win", align_bytes=64)
-        x_rows = x_words[0].rearrange("p c r -> p (c r)").bitcast(I32)
-        for h in range(2):
-            cols = slice(h * T // 2, (h + 1) * T // 2)
-            nc.sync.dma_start(out=xw_win[:, cols].bitcast(I32), in_=x_rows[:, cols])
         n3_l = load_list(n3, "n3_l")
+        wb_raw = [load_columns(wb, a, b, f"wb_raw{a}") for a, b in WB_LOADS[:2]]
         load_scale_rows(nc.sync, xs_win, x_scales[0])
-        wb_raw = [load_half(wb, h, f"wb_raw{h}") for h in range(2)]
-        wa_raw = [load_half(wa, h, f"wa_raw{h}") for h in range(2)]
+        wb_raw.append(load_columns(wb, *WB_LOADS[2], "wb_raw_last"))
+        xw_win = sb.tile([P, T], U32, name="xw_win", align_bytes=64)
+        nc.sync.dma_start(out=xw_win[:].bitcast(I32), in_=x_words[0].rearrange("p c r -> p (c r)").bitcast(I32))
+        wa_raw = [load_columns(wa, a, b, f"wa_raw{a}") for a, b in pieces(0, H)]
         w1w_raw = sb.tile([P, N], U32, name="w1w_raw", align_bytes=64)
         nc.sync.dma_start(out=w1w_raw[:].bitcast(I32), in_=w1_words[0].rearrange("p c r -> p (c r)").bitcast(I32))
         w1s_raw = sb.tile([P, N], U8, name="w1s_raw", align_bytes=64)
@@ -96,11 +96,6 @@ def tile_picked_twtpullbgshare_none_po_kernel(
         nc.vector.tensor_scalar(out=half_gate[:], in0=gate[:], scalar1=0.5, scalar2=None, op0=ALU.mult)
 
         ex = [sb.tile([P, H + SPARE], F32, name=f"ex{t}", align_bytes=64) for t in range(PACK)]
-        for t in range(PACK):
-            nc.gpsimd.memset(ex[t][:, H:], 0.0)
-        d_win = [sb.tile([P, 2 * H], F32, name=f"d_win{t}", align_bytes=64) for t in range(PACK)]
-        for t in range(PACK):
-            nc.gpsimd.memset(d_win[t][:, H:], 0.0)
         ident = sb.tile([P, P], F32, name="ident")
         make_identity(nc, ident[:])
 
@@ -109,8 +104,10 @@ def tile_picked_twtpullbgshare_none_po_kernel(
             nc.vector.tensor_copy(out=dealt(tile[:]), in_=window[:].indirect(offsets[:]))
             return tile
 
-        xw_two = pick(xw_win, two_l, U32, "xw_two")
         xs_two = pick(xs_win, two_l, U8, "xs_two")
+        xs_off = pick(xs_win, offs_l, U8, "xs_off")
+        xw_two = pick(xw_win, two_l, U32, "xw_two")
+        xw_off = pick(xw_win, offs_l, U32, "xw_off")
 
         def grouped_tile(name, cols):
             return sb.tile([P, cols, PACK], BF16, name=name, tag=name, align_bytes=64)
@@ -136,17 +133,15 @@ def tile_picked_twtpullbgshare_none_po_kernel(
         d_ps = [ps.tile([P, H], F32, name=f"d_ps{t}", tag=f"bank{t}") for t in range(PACK)]
         y_ps = [ps.tile([P, H], F32, name=f"y_ps{t}", tag=f"bank{PACK + t}") for t in range(PACK)]
 
-        round_scalar(wb_grp[:, :HALF], wb_raw[0][:])
-        round_vector(wb_grp[:, HALF:], wb_raw[1][:])
+        for (a, b), raw in zip(WB_LOADS, wb_raw):
+            round_scalar(wb_grp[:, a:b], raw[:])
         quantize(wb_codes[:], wb_scales[:], wb_grp[:])
         for t in range(PACK):
             product(d_ps[t][:], xw_two, xs_two, t, wb_codes[:], wb_scales[:])
-        xw_off = pick(xw_win, offs_l, U32, "xw_off", tag="wb_grp")
-        xs_off = pick(xs_win, offs_l, U8, "xs_off", tag="xs_two")
         round_gpsimd(wa_grp[:, :HALF], wa_raw[0][:])
-        round_vector(wa_grp[:, HALF:], wa_raw[1][:])
 
         def y_products():
+            round_vector(wa_grp[:, HALF:], wa_raw[1][:])
             quantize(wa_codes[:], wa_scales[:], wa_grp[:])
             for t in range(PACK):
                 product(y_ps[t][:], xw_off, xs_off, t, wa_codes[:], wa_scales[:])
@@ -157,39 +152,51 @@ def tile_picked_twtpullbgshare_none_po_kernel(
         def row_tile(name, tag=""):
             return sb.tile([P, H], F32, name=name, tag=tag or name, align_bytes=64)
 
-        def d_rows(t, tag=""):
-            if t < 2:
-                nc.scalar.copy(out=d_win[t][:, :H], in_=d_ps[t][:])
+        def d_rows(t, tag="", win_tag=""):
+            d_wide = sb.tile([P, 2 * H], F32, name=f"d_win{t}", tag=win_tag or f"d_win{t}", align_bytes=64)
+            d_win = d_wide[:, :H]
+            if t < 1:
+                nc.scalar.copy(out=d_win[:], in_=d_ps[t][:])
             else:
-                nc.vector.tensor_copy(out=d_win[t][:, :H], in_=d_ps[t][:])
+                nc.vector.tensor_copy(out=d_win[:], in_=d_ps[t][:])
             d_far = row_tile(f"d_far{t}", tag)
-            fetch(d_far[:], d_win[t], n2_l, 0, H)
+            fetch(d_far[:], d_wide, n2_l, 0, H)
             d_gap[t] = row_tile(f"d_gap{t}")
-            nc.gpsimd.tensor_tensor(out=d_gap[t][:], in0=d_far[:], in1=d_win[t][:, :H], op=ALU.subtract)
+            nc.gpsimd.tensor_tensor(out=d_gap[t][:], in0=d_far[:], in1=d_win[:], op=ALU.subtract)
 
-        def th_rows(t, tag=""):
-            th[t] = row_tile(f"th{t}", tag)
-            nc.scalar.activation(out=th[t][:], in_=d_gap[t][:], func=ACT.Tanh, scale=0.5)
+        def th_rows(t, a, b, tag=""):
+            tile = sb.tile([P, b - a], F32, name=f"th{t}_{a}", tag=tag or f"th{t}_{a}", align_bytes=64)
+            nc.scalar.activation(out=tile[:], in_=d_gap[t][:, a:b], func=ACT.Tanh, scale=0.5)
+            for s, e in pieces(a, b):
+                th[t, s // HALF] = tile[:, s - a : e - a]
 
         def y_rows(t, tag=""):
-            y_win[t] = row_tile(f"y_win{t}")
+            y_wide = sb.tile([P, 2 * H], F32, name=f"y_win{t}", align_bytes=64)
+            y_win[t] = y_wide[:, :H]
             nc.vector.tensor_scalar(out=y_win[t][:], in0=y_ps[t][:], scalar1=half_gate[:, t : t + 1], scalar2=None, op0=ALU.mult)
             y_far[t] = row_tile(f"y_far{t}", tag)
-            for s, e in pieces(0, H):
-                fetch(y_far[t][:, s:e], y_win[t], n1_l, s, e)
+            for s, e in pieces(0, H) if t == PACK - 1 else [(0, H)]:
+                fetch(y_far[t][:, s:e], y_wide, n1_l, s, e)
 
-        def halves(ap):
-            return ap.rearrange("p (h c) -> p h c", c=HALF)
+        y_gap, pull = {}, {}
 
-        def mix(step, t, a, b, early=None):
-            if early is None:
-                y_gap = sb.tile([P, b - a], F32, name=f"y_gap{step}", tag=f"mix{step % 2}")
-                nc.vector.scalar_tensor_tensor(out=y_gap[:], in0=y_ps[t][:, a:b], scalar=half_gate[:, t : t + 1], in1=y_far[t][:, a:b], op0=ALU.mult, op1=ALU.subtract)
-            else:
-                y_gap = early
-            pull = sb.tile([P, b - a], F32, name=f"pull{t}_{a}", tag=f"mix{(step + 1) % 2}")
-            nc.vector.scalar_tensor_tensor(out=pull[:], in0=th[t][:, a:b], scalar=1.0, in1=y_gap[:], op0=ALU.add, op1=ALU.mult)
-            nc.vector.scalar_tensor_tensor(out=z[:, a // HALF : b // HALF, t, :], in0=halves(y_ps[t][:, a:b]), scalar=gate[:, t : t + 1], in1=halves(pull[:]), op0=ALU.mult, op1=ALU.subtract)
+        def mix_gap(t, h):
+            cols = slice(h * HALF, (h + 1) * HALF)
+            y_gap[h] = sb.tile([P, HALF], F32, name=f"y_gap{h}")
+            nc.vector.scalar_tensor_tensor(out=y_gap[h][:], in0=y_ps[t][:, cols], scalar=half_gate[:, t : t + 1], in1=y_far[t][:, cols], op0=ALU.mult, op1=ALU.subtract)
+
+        def mix_pull(t, h):
+            pull[h] = sb.tile([P, HALF], F32, name=f"pull{h}")
+            nc.vector.scalar_tensor_tensor(out=pull[h][:], in0=th[t, h], scalar=1.0, in1=y_gap[h][:], op0=ALU.add, op1=ALU.mult)
+
+        def mix_out(t, h):
+            cols = slice(h * HALF, (h + 1) * HALF)
+            nc.vector.scalar_tensor_tensor(out=z[:, h, t, :], in0=y_ps[t][:, cols], scalar=gate[:, t : t + 1], in1=pull[h][:], op0=ALU.mult, op1=ALU.subtract)
+
+        def mix(t):
+            for step in (mix_gap, mix_pull, mix_out):
+                for h in range(2):
+                    step(t, h)
 
         def deal_w1():
             nc.gpsimd.tensor_copy(out=w1w[:].rearrange("p (t m) -> p t m", t=PACK), in_=w1w_raw[:].rearrange("p (m t) -> p t m", t=PACK))
@@ -198,67 +205,76 @@ def tile_picked_twtpullbgshare_none_po_kernel(
         d_rows(0)
         d_rows(1)
         y_products()
-        th_rows(0)
+        th_rows(0, 0, H)
         y_rows(0)
-        d_rows(2)
+        d_rows(2, "y_win0", "xs_off")
+        th_rows(1, 0, H)
         y_rows(1, "d_gap0")
-        th_rows(1, "y_win0")
-        d_rows(3, "y_win1")
-        w1w = sb.tile([P, N], U32, name="w1w", tag="wa_grp", align_bytes=64)
+        d_rows(3, "y_win1", "xw_off")
+        th_rows(2, 0, H)
+        y_rows(2, "d_gap1")
+        th_rows(3, 0, HALF)
+        y_rows(3, "d_gap2")
+        th_rows(3, HALF, H, "y_win3")
+        w1w = sb.tile([P, N], U32, name="w1w", tag="d_far0", align_bytes=64)
         w1s = sb.tile([P, N], U8, name="w1s", tag="d_far1", align_bytes=64)
         deal_w1()
-        mix(0, 0, 0, H)
-        y_rows(2, "d_gap1")
-        th_rows(2, "y_win2")
-        mix(1, 1, 0, H)
-        th_rows(3)
-        y_rows(3, "d_gap2")
-        mix(2, 2, 0, H)
-        z_grp = [grouped_tile(f"z_grp{h}", HALF) for h in range(2)]
+        mix(0)
+        mix(1)
+        mix(2)
+        z_grp = {}
         z_mx = [mx_tiles(f"z{h}", HALF) for h in range(2)]
         h_ps = [[ps.tile([P, HALF], F32, name=f"h_ps{h}_{t}", tag=f"bank{PACK * h + t}") for t in range(PACK)] for h in range(2)]
-
-        def places(h):
-            round_vector(z_grp[h][:], z[:, h])
-            quantize(z_mx[h][0][:], z_mx[h][1][:], z_grp[h][:])
-            for t in range(PACK):
-                product(h_ps[h][t][:], w1w, w1s, t, z_mx[h][0][:], z_mx[h][1][:])
 
         def exp_rows(t, h):
             nc.scalar.activation(out=ex[t][:, h * HALF : (h + 1) * HALF], in_=h_ps[h][t][:], func=ACT.Exp, scale=0.5)
 
-        late_gap = sb.tile([P, H], F32, name="late_gap")
-        for s, e in pieces(0, H):
-            nc.gpsimd.tensor_tensor(out=late_gap[:, s:e], in0=y_win[3][:, s:e], in1=y_far[3][:, s:e], op=ALU.subtract)
-        mix(2, 3, 0, HALF, early=late_gap[:, :HALF])
+        def places(h):
+            quantize(z_mx[h][0][:], z_mx[h][1][:], z_grp[h][:])
+            for t in range(PACK):
+                product(h_ps[h][t][:], w1w, w1s, t, z_mx[h][0][:], z_mx[h][1][:])
+
+        mix_gap(3, 0)
+        mix_pull(3, 0)
+        mix_gap(3, 1)
+        mix_out(3, 0)
+        mix_pull(3, 1)
+        z_grp[0] = grouped_tile("z_grp", HALF)
+        round_vector(z_grp[0][:], z[:, 0])
+        mix_out(3, 1)
         places(0)
+        z_grp[1] = grouped_tile("z_grp", HALF)
+        round_vector(z_grp[1][:], z[:, 1])
+        places(1)
         for t in range(PACK):
             exp_rows(t, 0)
-        mix(2, 3, HALF, H, early=late_gap[:, HALF:])
-        places(1)
 
         out_rows = out_0.rearrange("(p t) j -> p t j", t=PACK)
         out_words = out_1[0].rearrange("p c r -> p (c r)").bitcast(I32)
         o_scales = sb.tile([P, H], U8, name="o_scales", align_bytes=64)
         res = [sb.tile([P, PACK, b - a], F32, name=f"res{c}") for c, (a, b) in enumerate(OUT_CHUNKS)]
         last = len(OUT_CHUNKS) - 1
-        blocks = []
-        for c, (a, b) in enumerate(OUT_CHUNKS):
-            rows = P // (b - a)
-            for first in range(0, PACK, rows):
-                blocks.append((c, first, rows))
-        turned = blocks[:-1]
         held = {}
 
-        def members(c, first, rows):
-            a, b = OUT_CHUNKS[c]
-            mb = sb.tile([P, rows, (b - a) * MEMBERS], F32, name=f"mb{c}_{first}", tag="mb", bufs=3)
-            for e in range(rows):
-                fetch(mb[:, e, :], ex[first + e], n3_l, a * MEMBERS, b * MEMBERS, scale=0.25, bias=0.03125)
-            return mb[:].rearrange("p e (j m) -> p (e j) m", m=MEMBERS)
+        def members(t, a, b, into):
+            fetch(into, ex[t], n3_l, a * MEMBERS, b * MEMBERS, scale=0.25, bias=0.03125)
+
+        blocks = []
+        for c, (a, b) in enumerate(OUT_CHUNKS[:TURNED]):
+            runs = [(t, s, min(s + P, b)) for t in range(PACK) for s in range(a, b, P)]
+            per = P // min(P, b - a)
+            blocks.extend((c, runs[i : i + per]) for i in range(0, len(runs), per))
 
         def turned_sums(k):
-            mb = members(*turned[k])
+            c, runs = blocks[k]
+            a, b = OUT_CHUNKS[c]
+            if runs[0][1] == a:
+                held["mb"] = sb.tile([P, max(P, b - a) * MEMBERS], F32, name=f"mb{k}", tag="mb", bufs=3)
+                for e, (t, s, u) in enumerate(runs):
+                    n = (b - a) * MEMBERS
+                    members(t, a, b, held["mb"][:, e * n : (e + 1) * n])
+            first = (runs[0][1] - a) * MEMBERS
+            mb = held["mb"][:, first : first + P * MEMBERS].rearrange("p (j m) -> p j m", m=MEMBERS)
             den = ps.tile([P, P], F32, name=f"den{k}", tag=f"bank{PACK + k % 3}")
             for m in range(MEMBERS):
                 nc.tensor.matmul(den[:], lhsT=mb[:, :, m], rhs=ident[:], is_transpose=True, start=(m == 0), stop=(m == MEMBERS - 1))
@@ -275,13 +291,12 @@ def tile_picked_twtpullbgshare_none_po_kernel(
             held[k, "back"] = back
 
         def turned_res(k):
-            c, first, rows = turned[k]
+            c, runs = blocks[k]
             a, b = OUT_CHUNKS[c]
-            for e in range(rows):
-                t = first + e
-                nc.vector.tensor_tensor(out=res[c][:, t, :], in0=held[k, "back"][:, e * (b - a) : (e + 1) * (b - a)], in1=ex[t][:, a:b], op=ALU.mult)
-            if first + rows == PACK:
-                planes(c, round_vector)
+            for e, (t, s, u) in enumerate(runs):
+                nc.vector.tensor_tensor(out=res[c][:, t, s - a : u - a], in0=held[k, "back"][:, e * (u - s) : (e + 1) * (u - s)], in1=ex[t][:, s:u], op=ALU.mult)
+            if runs[-1][0] == PACK - 1 and runs[-1][2] == b:
+                planes(c, round_vector if c == last else round_gpsimd)
 
         def planes(c, rounding):
             a, b = OUT_CHUNKS[c]
@@ -292,49 +307,43 @@ def tile_picked_twtpullbgshare_none_po_kernel(
             quantize(o_codes[:], o_scales[:, a:b], o_grp[:])
             nc.sync.dma_start(out=out_words[:, a:b], in_=o_codes[:].bitcast(I32))
 
-        def straight_sums(t):
+        def straight(t, step):
             a, b = OUT_CHUNKS[last]
-            mb = members(last, t, 1)
-            twos = sb.tile([P, b - a, 2], F32, name=f"twos{t}")
-            nc.vector.tensor_tensor(out=twos[:], in0=mb[:, :, 0:2], in1=mb[:, :, 2:4], op=ALU.add)
-            held[t, "twos"] = twos
+            n = b - a
+            if step == 0:
+                mb = sb.tile([P, n, MEMBERS], F32, name=f"mb_last{t}", tag="mb", bufs=3)
+                members(t, a, b, mb[:].rearrange("p j m -> p (j m)"))
+                held[t, 0] = sb.tile([P, n, 2], F32, name=f"twos{t}")
+                nc.vector.tensor_tensor(out=held[t, 0][:], in0=mb[:, :, 0:2], in1=mb[:, :, 2:4], op=ALU.add)
+            elif step == 1:
+                held[t, 1] = sb.tile([P, n], F32, name=f"last_den{t}")
+                nc.vector.tensor_tensor(out=held[t, 1][:], in0=held[t, 0][:, :, 0], in1=held[t, 0][:, :, 1], op=ALU.add)
+            elif step == 2:
+                held[t, 2] = sb.tile([P, n], F32, name=f"last_rec{t}")
+                nc.vector.reciprocal(out=held[t, 2][:], in_=held[t, 1][:])
+            else:
+                nc.vector.tensor_tensor(out=res[last][:, t, :], in0=held[t, 2][:], in1=ex[t][:, a:b], op=ALU.mult)
 
-        def straight_den(t):
-            a, b = OUT_CHUNKS[last]
-            den = sb.tile([P, b - a], F32, name=f"straight_den{t}")
-            nc.vector.tensor_tensor(out=den[:], in0=held[t, "twos"][:, :, 0], in1=held[t, "twos"][:, :, 1], op=ALU.add)
-            held[t, "straight_den"] = den
-
-        def straight_rec(t):
-            a, b = OUT_CHUNKS[last]
-            rec = sb.tile([P, b - a], F32, name=f"straight_rec{t}")
-            nc.vector.reciprocal(out=rec[:], in_=held[t, "straight_den"][:])
-            held[t, "straight_rec"] = rec
-
-        def straight_res(t):
-            a, b = OUT_CHUNKS[last]
-            nc.vector.tensor_tensor(out=res[last][:, t, :], in0=held[t, "straight_rec"][:], in1=ex[t][:, a:b], op=ALU.mult)
-
-        for k in range(len(turned)):
-            if k < PACK:
-                exp_rows(k, 1)
+        seen = set()
+        for k in range(len(blocks)):
+            t = blocks[k][1][0][0]
+            if t not in seen:
+                seen.add(t)
+                exp_rows(t, 1)
             turned_sums(k)
             if k > 0:
                 turned_back(k - 1)
             turned_rec(k)
             if k > 0:
                 turned_res(k - 1)
-        end = len(turned) - 1
+        end = len(blocks) - 1
         turned_back(end)
-        straight_sums(2)
-        straight_sums(3)
-        straight_den(2)
-        straight_den(3)
-        straight_rec(2)
         turned_res(end)
-        straight_rec(3)
-        straight_res(2)
-        straight_res(3)
-        planes(last, round_vector)
+        if TURNED == last:
+            for wave in range(PACK + 3):
+                for t in range(PACK):
+                    if 0 <= wave - t < 4:
+                        straight(t, wave - t)
+            planes(last, round_vector)
         for q in range(4):
             nc.scalar.dma_start(out=out_2[0, 4 * q : 4 * q + 4, :].bitcast(I32), in_=o_scales[32 * q : 32 * q + 4, :].bitcast(I32))

@@ -19,11 +19,12 @@ FLOPS = 2 * (2 * K * S * H + S * N * H)
 P = 128
 PACK = 4
 HALF = H // 2
+HALVES = ((0, HALF), (HALF, H))
 MEMBERS = W // H
-SPARE = 32
 WB_LOADS = ((0, 256), (256, 384), (384, 512))
-OUT_CHUNKS = ((0, 128), (128, 256), (256, 384), (384, 512))
-TURNED = 4
+OUT_CHUNKS = ((0, 256), (256, 384), (384, 512))
+EX_WINDOW = 256 * MEMBERS + 32
+SUM_BANKS = 3
 
 
 def tile_picked_twtpullbgshare_none_po_kernel(
@@ -40,36 +41,69 @@ def tile_picked_twtpullbgshare_none_po_kernel(
             nc.sync.dma_start(out=tile[:], in_=src)
             return tile
 
-        def load_scale_rows(queue, tile, rows):
+        def load_scale_rows(tile, rows):
             for q in range(4):
-                queue.dma_start(out=tile[32 * q : 32 * q + 4, :].bitcast(I32), in_=rows[4 * q : 4 * q + 4, :].bitcast(I32))
+                nc.sync.dma_start(
+                    out=tile[32 * q : 32 * q + 4, :].bitcast(I32), in_=rows[4 * q : 4 * q + 4, :].bitcast(I32)
+                )
 
-        def dealt(ap):
-            return ap.rearrange("p (t m) -> p m t", t=PACK)
+        def load_words(words, cols, name):
+            tile = sb.tile([P, cols], U32, name=name, align_bytes=64)
+            nc.sync.dma_start(out=tile[:].bitcast(I32), in_=words.rearrange("p c r -> p (c r)").bitcast(I32))
+            return tile
 
         def load_columns(w, a, b, name):
             raw = sb.tile([P, PACK, b - a], F32, name=name, align_bytes=64)
             nc.sync.dma_start(out=raw[:], in_=w.rearrange("(p j) n -> p j n", j=PACK)[:, :, a:b])
             return raw
 
-        def weave(dst, src):
+        def grouped_tile(name, cols):
+            return sb.tile([P, cols, PACK], BF16, name=name, align_bytes=64)
+
+        def mx_tiles(name, cols):
+            codes = sb.tile([P, cols], U32, name=name + "_codes", align_bytes=64)
+            scales = sb.tile([P, cols], U8, name=name + "_scales", align_bytes=64)
+            return codes, scales
+
+        def by_fours(dst, src):
             return dst.rearrange("p (c i) t -> p c t i", i=4), src.rearrange("p t (c i) -> p c t i", i=4)
+
+        def group_on_scalar(dst, src):
+            dst, src = by_fours(dst, src)
+            nc.scalar.copy(out=dst, in_=src)
+
+        def group_on_vector(dst, src):
+            dst, src = by_fours(dst, src)
+            nc.vector.tensor_copy(out=dst, in_=src)
+
+        def group_on_gpsimd(dst, src):
+            nc.gpsimd.tensor_scalar(
+                out=dst, in0=src.rearrange("p t c -> p c t"), scalar1=1.0, scalar2=0.0, op0=ALU.mult, op1=ALU.add
+            )
 
         def quantize(codes, scales, grouped):
             nc.vector.quantize_mx(out=codes.bitcast(FP8X4), scales=scales, in_=grouped.rearrange("p c t -> p (c t)"))
 
-        def product(out, lhs_words, lhs_scales, t, codes, scales):
+        def product(out, words, word_scales, t, codes, scales):
             rows = slice(t * P, (t + 1) * P)
             nc.tensor.matmul_mx(
-                out=out, lhsT=lhs_words[:, rows].bitcast(FP8X4), lhsT_scale=lhs_scales[:, rows],
-                rhs=codes.bitcast(FP8X4), rhs_scale=scales, start=True, stop=True,
+                out=out,
+                lhsT=words[:, rows].bitcast(FP8X4),
+                lhsT_scale=word_scales[:, rows],
+                rhs=codes.bitcast(FP8X4),
+                rhs_scale=scales,
+                start=True,
+                stop=True,
             )
 
         def fetch(out, window, offsets, first, last, scale=1.0, bias=0.0):
-            nc.scalar.activation(out=out, in_=window[:].indirect(offsets[:, first // 16 : last // 16]), func=ACT.Copy, scale=scale, bias=bias)
-
-        def pieces(a, b):
-            return [(s, min(s + HALF, b)) for s in range(a, b, HALF)]
+            nc.scalar.activation(
+                out=out,
+                in_=window[:].indirect(offsets[:, first // 16 : last // 16]),
+                func=ACT.Copy,
+                scale=scale,
+                bias=bias,
+            )
 
         xs_win = sb.tile([P, T], U8, name="xs_win", align_bytes=64)
         nc.vector.memset(xs_win[:].bitcast(I32), 0)
@@ -80,28 +114,28 @@ def tile_picked_twtpullbgshare_none_po_kernel(
         n2_l = load_list(n2, "n2_l")
         n1_l = load_list(n1, "n1_l")
         n3_l = load_list(n3, "n3_l")
-        wb_raw = [load_columns(wb, a, b, f"wb_raw{a}") for a, b in WB_LOADS[:2]]
-        load_scale_rows(nc.sync, xs_win, x_scales[0])
-        wb_raw.append(load_columns(wb, *WB_LOADS[2], "wb_raw_last"))
-        xw_win = sb.tile([P, T], U32, name="xw_win", align_bytes=64)
-        nc.sync.dma_start(out=xw_win[:].bitcast(I32), in_=x_words[0].rearrange("p c r -> p (c r)").bitcast(I32))
-        wa_raw = [load_columns(wa, a, b, f"wa_raw{a}") for a, b in pieces(0, H)]
-        w1w_raw = sb.tile([P, N], U32, name="w1w_raw", align_bytes=64)
-        nc.sync.dma_start(out=w1w_raw[:].bitcast(I32), in_=w1_words[0].rearrange("p c r -> p (c r)").bitcast(I32))
+        wb_raw = [load_columns(wb, a, b, f"wb_raw{a}") for a, b in WB_LOADS[:-1]]
+        load_scale_rows(xs_win, x_scales[0])
+        wb_raw.append(load_columns(wb, *WB_LOADS[-1], "wb_raw_last"))
+        xw_win = load_words(x_words[0], T, "xw_win")
+        wa_raw = [load_columns(wa, a, b, f"wa_raw{a}") for a, b in HALVES]
+        w1w_raw = load_words(w1_words[0], N, "w1w_raw")
         w1s_raw = sb.tile([P, N], U8, name="w1s_raw", align_bytes=64)
         nc.gpsimd.memset(w1s_raw[:].bitcast(I32), 0)
-        load_scale_rows(nc.sync, w1s_raw, w1_scales[0])
+        load_scale_rows(w1s_raw, w1_scales[0])
 
         half_gate = sb.tile([P, PACK], F32, name="half_gate")
         nc.vector.tensor_scalar(out=half_gate[:], in0=gate[:], scalar1=0.5, scalar2=None, op0=ALU.mult)
 
-        ex = [sb.tile([P, H + SPARE], F32, name=f"ex{t}", align_bytes=64) for t in range(PACK)]
+        ex = [sb.tile([P, EX_WINDOW], F32, name=f"ex{t}", align_bytes=64) for t in range(PACK)]
         ident = sb.tile([P, P], F32, name="ident")
         make_identity(nc, ident[:])
 
-        def pick(window, offsets, dtype, name, tag=""):
-            tile = sb.tile([P, S], dtype, name=name, tag=tag or name, align_bytes=64)
-            nc.vector.tensor_copy(out=dealt(tile[:]), in_=window[:].indirect(offsets[:]))
+        def pick(window, offsets, dtype, name):
+            tile = sb.tile([P, S], dtype, name=name, align_bytes=64)
+            nc.vector.tensor_copy(
+                out=tile[:].rearrange("p (t m) -> p m t", t=PACK), in_=window[:].indirect(offsets[:])
+            )
             return tile
 
         xs_two = pick(xs_win, two_l, U8, "xs_two")
@@ -109,142 +143,116 @@ def tile_picked_twtpullbgshare_none_po_kernel(
         xw_two = pick(xw_win, two_l, U32, "xw_two")
         xw_off = pick(xw_win, offs_l, U32, "xw_off")
 
-        def grouped_tile(name, cols):
-            return sb.tile([P, cols, PACK], BF16, name=name, tag=name, align_bytes=64)
-
-        def mx_tiles(name, cols):
-            return (sb.tile([P, cols], U32, name=name + "_codes", align_bytes=64),
-                    sb.tile([P, cols], U8, name=name + "_scales", align_bytes=64))
-
-        def round_scalar(dst, src):
-            o, i = weave(dst, src)
-            nc.scalar.copy(out=o, in_=i)
-
-        def round_vector(dst, src):
-            o, i = weave(dst, src)
-            nc.vector.tensor_copy(out=o, in_=i)
-
-        def round_gpsimd(dst, src):
-            nc.gpsimd.tensor_scalar(out=dst, in0=src.rearrange("p t c -> p c t"), scalar1=1.0, scalar2=0.0, op0=ALU.mult, op1=ALU.add)
-
-        wb_grp, wa_grp = grouped_tile("wb_grp", H), grouped_tile("wa_grp", H)
+        wb_grp = grouped_tile("wb_grp", H)
+        wa_grp = [grouped_tile(f"wa_grp{h}", HALF) for h in range(2)]
         wb_codes, wb_scales = mx_tiles("wb", H)
         wa_codes, wa_scales = mx_tiles("wa", H)
         d_ps = [ps.tile([P, H], F32, name=f"d_ps{t}", tag=f"bank{t}") for t in range(PACK)]
         y_ps = [ps.tile([P, H], F32, name=f"y_ps{t}", tag=f"bank{PACK + t}") for t in range(PACK)]
 
         for (a, b), raw in zip(WB_LOADS, wb_raw):
-            round_scalar(wb_grp[:, a:b], raw[:])
+            group_on_scalar(wb_grp[:, a:b], raw[:])
         quantize(wb_codes[:], wb_scales[:], wb_grp[:])
         for t in range(PACK):
             product(d_ps[t][:], xw_two, xs_two, t, wb_codes[:], wb_scales[:])
-        round_gpsimd(wa_grp[:, :HALF], wa_raw[0][:])
-
-        def y_products():
-            round_vector(wa_grp[:, HALF:], wa_raw[1][:])
-            quantize(wa_codes[:], wa_scales[:], wa_grp[:])
-            for t in range(PACK):
-                product(y_ps[t][:], xw_off, xs_off, t, wa_codes[:], wa_scales[:])
+        group_on_gpsimd(wa_grp[0][:], wa_raw[0][:])
 
         z = sb.tile([P, 2, PACK, HALF], BF16, name="z", align_bytes=64)
-        y_win, y_far, d_gap, th = {}, {}, {}, {}
+        d_gap, y_win = {}, {}
 
-        def row_tile(name, tag=""):
-            return sb.tile([P, H], F32, name=name, tag=tag or name, align_bytes=64)
-
-        def d_rows(t, tag="", win_tag=""):
-            d_wide = sb.tile([P, 2 * H], F32, name=f"d_win{t}", tag=win_tag or f"d_win{t}", align_bytes=64)
-            d_win = d_wide[:, :H]
-            if t < 1:
-                nc.scalar.copy(out=d_win[:], in_=d_ps[t][:])
+        def d_rows(t, tag):
+            window = sb.tile([P, 2 * H], F32, name=f"d_win{t}", tag=tag, align_bytes=64)
+            if t == 0:
+                nc.scalar.copy(out=window[:, :H], in_=d_ps[t][:])
             else:
-                nc.vector.tensor_copy(out=d_win[:], in_=d_ps[t][:])
-            d_far = row_tile(f"d_far{t}", tag)
-            fetch(d_far[:], d_wide, n2_l, 0, H)
-            d_gap[t] = row_tile(f"d_gap{t}")
-            nc.gpsimd.tensor_tensor(out=d_gap[t][:], in0=d_far[:], in1=d_win[:], op=ALU.subtract)
+                nc.vector.tensor_copy(out=window[:, :H], in_=d_ps[t][:])
+            d_far = sb.tile([P, H], F32, name=f"d_far{t}", align_bytes=64)
+            fetch(d_far[:], window, n2_l, 0, H)
+            d_gap[t] = sb.tile([P, H], F32, name=f"d_gap{t}")
+            nc.gpsimd.tensor_tensor(out=d_gap[t][:], in0=d_far[:], in1=window[:, :H], op=ALU.subtract)
 
-        def th_rows(t, a, b, tag=""):
-            tile = sb.tile([P, b - a], F32, name=f"th{t}_{a}", tag=tag or f"th{t}_{a}", align_bytes=64)
-            nc.scalar.activation(out=tile[:], in_=d_gap[t][:, a:b], func=ACT.Tanh, scale=0.5)
-            for s, e in pieces(a, b):
-                th[t, s // HALF] = tile[:, s - a : e - a]
+        for t in range(PACK - 1):
+            d_rows(t, f"d_win{t}")
+        group_on_vector(wa_grp[1][:], wa_raw[1][:])
+        for (a, b), grouped in zip(HALVES, wa_grp):
+            quantize(wa_codes[:, a:b], wa_scales[:, a:b], grouped[:])
+        for t in range(PACK):
+            product(y_ps[t][:], xw_off, xs_off, t, wa_codes[:], wa_scales[:])
+        d_rows(PACK - 1, "wa_grp1")
+        for t in range(PACK):
+            y_win[t] = sb.tile([P, H], F32, name=f"y_win{t}", align_bytes=64)
+            nc.vector.tensor_scalar(
+                out=y_win[t][:], in0=y_ps[t][:], scalar1=half_gate[:, t : t + 1], scalar2=None, op0=ALU.mult
+            )
 
-        def y_rows(t, tag=""):
-            y_wide = sb.tile([P, 2 * H], F32, name=f"y_win{t}", align_bytes=64)
-            y_win[t] = y_wide[:, :H]
-            nc.vector.tensor_scalar(out=y_win[t][:], in0=y_ps[t][:], scalar1=half_gate[:, t : t + 1], scalar2=None, op0=ALU.mult)
-            y_far[t] = row_tile(f"y_far{t}", tag)
-            for s, e in pieces(0, H) if t == PACK - 1 else [(0, H)]:
-                fetch(y_far[t][:, s:e], y_wide, n1_l, s, e)
-
-        y_gap, pull = {}, {}
-
-        def mix_gap(t, h):
-            cols = slice(h * HALF, (h + 1) * HALF)
-            y_gap[h] = sb.tile([P, HALF], F32, name=f"y_gap{h}")
-            nc.vector.scalar_tensor_tensor(out=y_gap[h][:], in0=y_ps[t][:, cols], scalar=half_gate[:, t : t + 1], in1=y_far[t][:, cols], op0=ALU.mult, op1=ALU.subtract)
-
-        def mix_pull(t, h):
-            pull[h] = sb.tile([P, HALF], F32, name=f"pull{h}")
-            nc.vector.scalar_tensor_tensor(out=pull[h][:], in0=th[t, h], scalar=1.0, in1=y_gap[h][:], op0=ALU.add, op1=ALU.mult)
-
-        def mix_out(t, h):
-            cols = slice(h * HALF, (h + 1) * HALF)
-            nc.vector.scalar_tensor_tensor(out=z[:, h, t, :], in0=y_ps[t][:, cols], scalar=gate[:, t : t + 1], in1=pull[h][:], op0=ALU.mult, op1=ALU.subtract)
-
-        def mix(t):
-            for step in (mix_gap, mix_pull, mix_out):
-                for h in range(2):
-                    step(t, h)
-
-        def deal_w1():
-            nc.gpsimd.tensor_copy(out=w1w[:].rearrange("p (t m) -> p t m", t=PACK), in_=w1w_raw[:].rearrange("p (m t) -> p t m", t=PACK))
-            nc.gpsimd.tensor_copy(out=w1s[:].rearrange("p (t m) -> p t m", t=PACK), in_=w1s_raw[:].rearrange("p (m t) -> p t m", t=PACK))
-
-        d_rows(0)
-        d_rows(1)
-        y_products()
-        th_rows(0, 0, H)
-        y_rows(0)
-        d_rows(2, "y_win0", "xs_off")
-        th_rows(1, 0, H)
-        y_rows(1, "d_gap0")
-        d_rows(3, "y_win1", "xw_off")
-        th_rows(2, 0, H)
-        y_rows(2, "d_gap1")
-        th_rows(3, 0, HALF)
-        y_rows(3, "d_gap2")
-        th_rows(3, HALF, H, "y_win3")
         w1w = sb.tile([P, N], U32, name="w1w", tag="d_far0", align_bytes=64)
         w1s = sb.tile([P, N], U8, name="w1s", tag="d_far1", align_bytes=64)
-        deal_w1()
-        mix(0)
-        mix(1)
-        mix(2)
-        z_grp = {}
-        z_mx = [mx_tiles(f"z{h}", HALF) for h in range(2)]
-        h_ps = [[ps.tile([P, HALF], F32, name=f"h_ps{h}_{t}", tag=f"bank{PACK * h + t}") for t in range(PACK)] for h in range(2)]
+        for dealt, raw in ((w1w, w1w_raw), (w1s, w1s_raw)):
+            nc.gpsimd.tensor_copy(
+                out=dealt[:].rearrange("p (t m) -> p t m", t=PACK), in_=raw[:].rearrange("p (m t) -> p t m", t=PACK)
+            )
 
-        def exp_rows(t, h):
-            nc.scalar.activation(out=ex[t][:, h * HALF : (h + 1) * HALF], in_=h_ps[h][t][:], func=ACT.Exp, scale=0.5)
+        steps = [(h, t) for h in range(2) for t in range(PACK)]
+        y_gap, th, pull = {}, {}, {}
+
+        def half_tile(name):
+            return sb.tile([P, HALF], F32, name=name, bufs=2)
+
+        def mix_gap(k):
+            h, t = steps[k]
+            a, b = HALVES[h]
+            y_far = half_tile("y_far")
+            fetch(y_far[:], y_win[t], n1_l, a, b)
+            th[k] = half_tile("th")
+            nc.scalar.activation(out=th[k][:], in_=d_gap[t][:, a:b], func=ACT.Tanh, scale=0.5)
+            y_gap[k] = half_tile("y_gap")
+            nc.vector.scalar_tensor_tensor(
+                out=y_gap[k][:], in0=y_ps[t][:, a:b], scalar=half_gate[:, t : t + 1], in1=y_far[:],
+                op0=ALU.mult, op1=ALU.subtract,
+            )
+
+        def mix_pull(k):
+            pull[k] = half_tile("pull")
+            nc.vector.scalar_tensor_tensor(
+                out=pull[k][:], in0=th[k][:], scalar=1.0, in1=y_gap[k][:], op0=ALU.add, op1=ALU.mult
+            )
+
+        def mix_out(k):
+            h, t = steps[k]
+            a, b = HALVES[h]
+            nc.vector.scalar_tensor_tensor(
+                out=z[:, h, t, :], in0=y_ps[t][:, a:b], scalar=gate[:, t : t + 1], in1=pull[k][:],
+                op0=ALU.mult, op1=ALU.subtract,
+            )
+
+        z_grp = [grouped_tile(f"z_grp{h}", HALF) for h in range(2)]
+        z_mx = [mx_tiles(f"z{h}", HALF) for h in range(2)]
+        h_ps = [
+            [ps.tile([P, HALF], F32, name=f"h_ps{h}_{t}", tag=f"bank{PACK * h + t}") for t in range(PACK)]
+            for h in range(2)
+        ]
 
         def places(h):
-            quantize(z_mx[h][0][:], z_mx[h][1][:], z_grp[h][:])
+            codes, scales = z_mx[h]
+            quantize(codes[:], scales[:], z_grp[h][:])
             for t in range(PACK):
-                product(h_ps[h][t][:], w1w, w1s, t, z_mx[h][0][:], z_mx[h][1][:])
+                product(h_ps[h][t][:], w1w, w1s, t, codes[:], scales[:])
 
-        mix_gap(3, 0)
-        mix_pull(3, 0)
-        mix_gap(3, 1)
-        mix_out(3, 0)
-        mix_pull(3, 1)
-        z_grp[0] = grouped_tile("z_grp", HALF)
-        round_vector(z_grp[0][:], z[:, 0])
-        mix_out(3, 1)
-        places(0)
-        z_grp[1] = grouped_tile("z_grp", HALF)
-        round_vector(z_grp[1][:], z[:, 1])
+        def exp_rows(t, h):
+            a, b = HALVES[h]
+            nc.scalar.activation(out=ex[t][:, a:b], in_=h_ps[h][t][:], func=ACT.Exp, scale=0.5)
+
+        for k in range(len(steps)):
+            mix_gap(k)
+            if k > 0:
+                mix_out(k - 1)
+            mix_pull(k)
+            if k == PACK:
+                group_on_vector(z_grp[0][:], z[:, 0])
+            if k == PACK + 1:
+                places(0)
+        mix_out(len(steps) - 1)
+        group_on_vector(z_grp[1][:], z[:, 1])
         places(1)
         for t in range(PACK):
             exp_rows(t, 0)
@@ -253,97 +261,67 @@ def tile_picked_twtpullbgshare_none_po_kernel(
         out_words = out_1[0].rearrange("p c r -> p (c r)").bitcast(I32)
         o_scales = sb.tile([P, H], U8, name="o_scales", align_bytes=64)
         res = [sb.tile([P, PACK, b - a], F32, name=f"res{c}") for c, (a, b) in enumerate(OUT_CHUNKS)]
-        last = len(OUT_CHUNKS) - 1
-        held = {}
+        patches = [
+            (c, t, first) for c, (a, b) in enumerate(OUT_CHUNKS) for t in range(PACK) for first in range(a, b, P)
+        ]
+        members, sums, recs, turned = {}, {}, {}, {}
 
-        def members(t, a, b, into):
-            fetch(into, ex[t], n3_l, a * MEMBERS, b * MEMBERS, scale=0.25, bias=0.03125)
-
-        blocks = []
-        for c, (a, b) in enumerate(OUT_CHUNKS[:TURNED]):
-            runs = [(t, s, min(s + P, b)) for t in range(PACK) for s in range(a, b, P)]
-            per = P // min(P, b - a)
-            blocks.extend((c, runs[i : i + per]) for i in range(0, len(runs), per))
-
-        def turned_sums(k):
-            c, runs = blocks[k]
+        def patch_sums(k):
+            c, t, first = patches[k]
             a, b = OUT_CHUNKS[c]
-            if runs[0][1] == a:
-                held["mb"] = sb.tile([P, max(P, b - a) * MEMBERS], F32, name=f"mb{k}", tag="mb", bufs=3)
-                for e, (t, s, u) in enumerate(runs):
-                    n = (b - a) * MEMBERS
-                    members(t, a, b, held["mb"][:, e * n : (e + 1) * n])
-            first = (runs[0][1] - a) * MEMBERS
-            mb = held["mb"][:, first : first + P * MEMBERS].rearrange("p (j m) -> p j m", m=MEMBERS)
-            den = ps.tile([P, P], F32, name=f"den{k}", tag=f"bank{PACK + k % 3}")
+            if first == a:
+                if c == 0:
+                    exp_rows(t, 1)
+                members[c, t] = sb.tile([P, (b - a) * MEMBERS], F32, name=f"mb{k}", tag="mb", bufs=3)
+                fetch(members[c, t][:], ex[t], n3_l, a * MEMBERS, b * MEMBERS, scale=0.25, bias=0.03125)
+            start = (first - a) * MEMBERS
+            mb = members[c, t][:, start : start + P * MEMBERS].rearrange("p (j m) -> p j m", m=MEMBERS)
+            sums[k] = ps.tile([P, P], F32, name=f"sums{k}", tag=f"bank{PACK + k % SUM_BANKS}")
             for m in range(MEMBERS):
-                nc.tensor.matmul(den[:], lhsT=mb[:, :, m], rhs=ident[:], is_transpose=True, start=(m == 0), stop=(m == MEMBERS - 1))
-            held[k, "den"] = den
+                nc.tensor.matmul(
+                    sums[k][:], lhsT=mb[:, :, m], rhs=ident[:], is_transpose=True,
+                    start=(m == 0), stop=(m == MEMBERS - 1),
+                )
 
-        def turned_rec(k):
-            rec = sb.tile([P, P], F32, name=f"rec{k}")
-            nc.vector.reciprocal(out=rec[:], in_=held[k, "den"][:])
-            held[k, "rec"] = rec
+        def patch_reciprocal(k):
+            recs[k] = sb.tile([P, P], F32, name=f"rec{k}")
+            nc.vector.reciprocal(out=recs[k][:], in_=sums[k][:])
 
-        def turned_back(k):
-            back = ps.tile([P, P], F32, name=f"back{k}", tag=f"bank{k % PACK}")
-            nc.tensor.transpose(back[:], held[k, "rec"][:], ident[:])
-            held[k, "back"] = back
+        def patch_turn_back(k):
+            turned[k] = ps.tile([P, P], F32, name=f"turned{k}", tag=f"bank{k % PACK}")
+            nc.tensor.transpose(turned[k][:], recs[k][:], ident[:])
 
-        def turned_res(k):
-            c, runs = blocks[k]
+        def patch_result(k):
+            c, t, first = patches[k]
             a, b = OUT_CHUNKS[c]
-            for e, (t, s, u) in enumerate(runs):
-                nc.vector.tensor_tensor(out=res[c][:, t, s - a : u - a], in0=held[k, "back"][:, e * (u - s) : (e + 1) * (u - s)], in1=ex[t][:, s:u], op=ALU.mult)
-            if runs[-1][0] == PACK - 1 and runs[-1][2] == b:
-                planes(c, round_vector if c == last else round_gpsimd)
+            nc.vector.tensor_tensor(
+                out=res[c][:, t, first - a : first - a + P], in0=turned[k][:], in1=ex[t][:, first : first + P],
+                op=ALU.mult,
+            )
+            if t == PACK - 1 and first + P == b:
+                planes(c)
 
-        def planes(c, rounding):
+        def planes(c):
             a, b = OUT_CHUNKS[c]
             nc.sync.dma_start(out=out_rows[:, :, a:b], in_=res[c][:])
             o_grp = grouped_tile(f"o_grp{c}", b - a)
-            rounding(o_grp[:], res[c][:])
+            group = group_on_vector if b == H else group_on_gpsimd
+            group(o_grp[:], res[c][:])
             o_codes = sb.tile([P, b - a], U32, name=f"o_codes{c}", align_bytes=64)
             quantize(o_codes[:], o_scales[:, a:b], o_grp[:])
             nc.sync.dma_start(out=out_words[:, a:b], in_=o_codes[:].bitcast(I32))
 
-        def straight(t, step):
-            a, b = OUT_CHUNKS[last]
-            n = b - a
-            if step == 0:
-                mb = sb.tile([P, n, MEMBERS], F32, name=f"mb_last{t}", tag="mb", bufs=3)
-                members(t, a, b, mb[:].rearrange("p j m -> p (j m)"))
-                held[t, 0] = sb.tile([P, n, 2], F32, name=f"twos{t}")
-                nc.vector.tensor_tensor(out=held[t, 0][:], in0=mb[:, :, 0:2], in1=mb[:, :, 2:4], op=ALU.add)
-            elif step == 1:
-                held[t, 1] = sb.tile([P, n], F32, name=f"last_den{t}")
-                nc.vector.tensor_tensor(out=held[t, 1][:], in0=held[t, 0][:, :, 0], in1=held[t, 0][:, :, 1], op=ALU.add)
-            elif step == 2:
-                held[t, 2] = sb.tile([P, n], F32, name=f"last_rec{t}")
-                nc.vector.reciprocal(out=held[t, 2][:], in_=held[t, 1][:])
-            else:
-                nc.vector.tensor_tensor(out=res[last][:, t, :], in0=held[t, 2][:], in1=ex[t][:, a:b], op=ALU.mult)
+        for k in range(len(patches)):
+            patch_sums(k)
+            if k > 0:
+                patch_turn_back(k - 1)
+            patch_reciprocal(k)
+            if k > 0:
+                patch_result(k - 1)
+        patch_turn_back(len(patches) - 1)
+        patch_result(len(patches) - 1)
 
-        seen = set()
-        for k in range(len(blocks)):
-            t = blocks[k][1][0][0]
-            if t not in seen:
-                seen.add(t)
-                exp_rows(t, 1)
-            turned_sums(k)
-            if k > 0:
-                turned_back(k - 1)
-            turned_rec(k)
-            if k > 0:
-                turned_res(k - 1)
-        end = len(blocks) - 1
-        turned_back(end)
-        turned_res(end)
-        if TURNED == last:
-            for wave in range(PACK + 3):
-                for t in range(PACK):
-                    if 0 <= wave - t < 4:
-                        straight(t, wave - t)
-            planes(last, round_vector)
         for q in range(4):
-            nc.scalar.dma_start(out=out_2[0, 4 * q : 4 * q + 4, :].bitcast(I32), in_=o_scales[32 * q : 32 * q + 4, :].bitcast(I32))
+            nc.scalar.dma_start(
+                out=out_2[0, 4 * q : 4 * q + 4, :].bitcast(I32), in_=o_scales[32 * q : 32 * q + 4, :].bitcast(I32)
+            )

from contextlib import ExitStack

import concourse.mybir as mybir
from concourse.masks import make_identity

F32 = mybir.dt.float32
BF16 = mybir.dt.bfloat16
I32 = mybir.dt.int32
U32 = mybir.dt.uint32
U16 = mybir.dt.uint16
U8 = mybir.dt.uint8
FP8X4 = mybir.dt.float8_e4m3fn_x4
ALU = mybir.AluOpType
ACT = mybir.ActivationFunctionType

K, T, S, N, H, W = 512, 2048, 512, 512, 512, 2048
FLOPS = 2 * (2 * K * S * H + S * N * H)

P = 128
PACK = 4
HALF = H // 2
HALVES = ((0, HALF), (HALF, H))
MEMBERS = W // H
WB_LOADS = ((0, 256), (256, 384), (384, 512))
OUT_CHUNKS = ((0, 256), (256, 384), (384, 512))
EX_WINDOW = 256 * MEMBERS + 32
SUM_BANKS = 3


def tile_picked_twtpullbgshare_none_po_kernel(
    tc, x_words, x_scales, wa, wb, gt, w1_words, w1_scales, offs, two, n1, n2, n3, out_0, out_1, out_2
):
    nc = tc.nc
    with ExitStack() as ctx:
        lists = ctx.enter_context(tc.tile_pool(name="lists", bufs=1))
        sb = ctx.enter_context(tc.tile_pool(name="sb", bufs=1))
        ps = ctx.enter_context(tc.psum_pool(name="ps", bufs=1))

        def load_list(src, name):
            tile = lists.tile(list(src.shape), U16, name=name)
            nc.sync.dma_start(out=tile[:], in_=src)
            return tile

        def load_scale_rows(tile, rows):
            for q in range(4):
                nc.sync.dma_start(
                    out=tile[32 * q : 32 * q + 4, :].bitcast(I32), in_=rows[4 * q : 4 * q + 4, :].bitcast(I32)
                )

        def load_words(words, cols, name):
            tile = sb.tile([P, cols], U32, name=name, align_bytes=64)
            nc.sync.dma_start(out=tile[:].bitcast(I32), in_=words.rearrange("p c r -> p (c r)").bitcast(I32))
            return tile

        def load_columns(w, a, b, name):
            raw = sb.tile([P, PACK, b - a], F32, name=name, align_bytes=64)
            nc.sync.dma_start(out=raw[:], in_=w.rearrange("(p j) n -> p j n", j=PACK)[:, :, a:b])
            return raw

        def grouped_tile(name, cols):
            return sb.tile([P, cols, PACK], BF16, name=name, align_bytes=64)

        def mx_tiles(name, cols):
            codes = sb.tile([P, cols], U32, name=name + "_codes", align_bytes=64)
            scales = sb.tile([P, cols], U8, name=name + "_scales", align_bytes=64)
            return codes, scales

        def by_fours(dst, src):
            return dst.rearrange("p (c i) t -> p c t i", i=4), src.rearrange("p t (c i) -> p c t i", i=4)

        def group_on_scalar(dst, src):
            dst, src = by_fours(dst, src)
            nc.scalar.copy(out=dst, in_=src)

        def group_on_vector(dst, src):
            dst, src = by_fours(dst, src)
            nc.vector.tensor_copy(out=dst, in_=src)

        def group_on_gpsimd(dst, src):
            nc.gpsimd.tensor_scalar(
                out=dst, in0=src.rearrange("p t c -> p c t"), scalar1=1.0, scalar2=0.0, op0=ALU.mult, op1=ALU.add
            )

        def quantize(codes, scales, grouped):
            nc.vector.quantize_mx(out=codes.bitcast(FP8X4), scales=scales, in_=grouped.rearrange("p c t -> p (c t)"))

        def product(out, words, word_scales, t, codes, scales):
            rows = slice(t * P, (t + 1) * P)
            nc.tensor.matmul_mx(
                out=out,
                lhsT=words[:, rows].bitcast(FP8X4),
                lhsT_scale=word_scales[:, rows],
                rhs=codes.bitcast(FP8X4),
                rhs_scale=scales,
                start=True,
                stop=True,
            )

        def fetch(out, window, offsets, first, last, scale=1.0, bias=0.0):
            nc.scalar.activation(
                out=out,
                in_=window[:].indirect(offsets[:, first // 16 : last // 16]),
                func=ACT.Copy,
                scale=scale,
                bias=bias,
            )

        xs_win = sb.tile([P, T], U8, name="xs_win", align_bytes=64)
        nc.vector.memset(xs_win[:].bitcast(I32), 0)
        two_l = load_list(two, "two_l")
        offs_l = load_list(offs, "offs_l")
        gate = sb.tile([P, PACK], F32, name="gate")
        nc.sync.dma_start(out=gate[:], in_=gt.rearrange("(p t) one -> p (t one)", t=PACK))
        n2_l = load_list(n2, "n2_l")
        n1_l = load_list(n1, "n1_l")
        n3_l = load_list(n3, "n3_l")
        wb_raw = [load_columns(wb, a, b, f"wb_raw{a}") for a, b in WB_LOADS[:-1]]
        load_scale_rows(xs_win, x_scales[0])
        wb_raw.append(load_columns(wb, *WB_LOADS[-1], "wb_raw_last"))
        xw_win = load_words(x_words[0], T, "xw_win")
        wa_raw = [load_columns(wa, a, b, f"wa_raw{a}") for a, b in HALVES]
        w1w_raw = load_words(w1_words[0], N, "w1w_raw")
        w1s_raw = sb.tile([P, N], U8, name="w1s_raw", align_bytes=64)
        nc.gpsimd.memset(w1s_raw[:].bitcast(I32), 0)
        load_scale_rows(w1s_raw, w1_scales[0])

        half_gate = sb.tile([P, PACK], F32, name="half_gate")
        nc.vector.tensor_scalar(out=half_gate[:], in0=gate[:], scalar1=0.5, scalar2=None, op0=ALU.mult)

        ex = [sb.tile([P, EX_WINDOW], F32, name=f"ex{t}", align_bytes=64) for t in range(PACK)]
        ident = sb.tile([P, P], F32, name="ident")
        make_identity(nc, ident[:])

        def pick(window, offsets, dtype, name):
            tile = sb.tile([P, S], dtype, name=name, align_bytes=64)
            nc.vector.tensor_copy(
                out=tile[:].rearrange("p (t m) -> p m t", t=PACK), in_=window[:].indirect(offsets[:])
            )
            return tile

        xs_two = pick(xs_win, two_l, U8, "xs_two")
        xs_off = pick(xs_win, offs_l, U8, "xs_off")
        xw_two = pick(xw_win, two_l, U32, "xw_two")
        xw_off = pick(xw_win, offs_l, U32, "xw_off")

        wb_grp = grouped_tile("wb_grp", H)
        wa_grp = [grouped_tile(f"wa_grp{h}", HALF) for h in range(2)]
        wb_codes, wb_scales = mx_tiles("wb", H)
        wa_codes, wa_scales = mx_tiles("wa", H)
        d_ps = [ps.tile([P, H], F32, name=f"d_ps{t}", tag=f"bank{t}") for t in range(PACK)]
        y_ps = [ps.tile([P, H], F32, name=f"y_ps{t}", tag=f"bank{PACK + t}") for t in range(PACK)]

        for (a, b), raw in zip(WB_LOADS, wb_raw):
            group_on_scalar(wb_grp[:, a:b], raw[:])
        quantize(wb_codes[:], wb_scales[:], wb_grp[:])
        for t in range(PACK):
            product(d_ps[t][:], xw_two, xs_two, t, wb_codes[:], wb_scales[:])
        group_on_gpsimd(wa_grp[0][:], wa_raw[0][:])

        z = sb.tile([P, 2, PACK, HALF], BF16, name="z", align_bytes=64)
        d_gap, y_win = {}, {}

        def d_rows(t, tag):
            window = sb.tile([P, 2 * H], F32, name=f"d_win{t}", tag=tag, align_bytes=64)
            if t == 0:
                nc.scalar.copy(out=window[:, :H], in_=d_ps[t][:])
            else:
                nc.vector.tensor_copy(out=window[:, :H], in_=d_ps[t][:])
            d_far = sb.tile([P, H], F32, name=f"d_far{t}", align_bytes=64)
            fetch(d_far[:], window, n2_l, 0, H)
            d_gap[t] = sb.tile([P, H], F32, name=f"d_gap{t}")
            nc.gpsimd.tensor_tensor(out=d_gap[t][:], in0=d_far[:], in1=window[:, :H], op=ALU.subtract)

        for t in range(PACK - 1):
            d_rows(t, f"d_win{t}")
        group_on_vector(wa_grp[1][:], wa_raw[1][:])
        for (a, b), grouped in zip(HALVES, wa_grp):
            quantize(wa_codes[:, a:b], wa_scales[:, a:b], grouped[:])
        for t in range(PACK):
            product(y_ps[t][:], xw_off, xs_off, t, wa_codes[:], wa_scales[:])
        d_rows(PACK - 1, "wa_grp1")
        for t in range(PACK):
            y_win[t] = sb.tile([P, H], F32, name=f"y_win{t}", align_bytes=64)
            nc.vector.tensor_scalar(
                out=y_win[t][:], in0=y_ps[t][:], scalar1=half_gate[:, t : t + 1], scalar2=None, op0=ALU.mult
            )

        w1w = sb.tile([P, N], U32, name="w1w", tag="d_far0", align_bytes=64)
        w1s = sb.tile([P, N], U8, name="w1s", tag="d_far1", align_bytes=64)
        for dealt, raw in ((w1w, w1w_raw), (w1s, w1s_raw)):
            nc.gpsimd.tensor_copy(
                out=dealt[:].rearrange("p (t m) -> p t m", t=PACK), in_=raw[:].rearrange("p (m t) -> p t m", t=PACK)
            )

        steps = [(h, t) for h in range(2) for t in range(PACK)]
        y_gap, th, pull = {}, {}, {}

        def half_tile(name):
            return sb.tile([P, HALF], F32, name=name, bufs=2)

        def mix_gap(k):
            h, t = steps[k]
            a, b = HALVES[h]
            y_far = half_tile("y_far")
            fetch(y_far[:], y_win[t], n1_l, a, b)
            th[k] = half_tile("th")
            nc.scalar.activation(out=th[k][:], in_=d_gap[t][:, a:b], func=ACT.Tanh, scale=0.5)
            y_gap[k] = half_tile("y_gap")
            nc.vector.scalar_tensor_tensor(
                out=y_gap[k][:], in0=y_ps[t][:, a:b], scalar=half_gate[:, t : t + 1], in1=y_far[:],
                op0=ALU.mult, op1=ALU.subtract,
            )

        def mix_pull(k):
            pull[k] = half_tile("pull")
            nc.vector.scalar_tensor_tensor(
                out=pull[k][:], in0=th[k][:], scalar=1.0, in1=y_gap[k][:], op0=ALU.add, op1=ALU.mult
            )

        def mix_out(k):
            h, t = steps[k]
            a, b = HALVES[h]
            nc.vector.scalar_tensor_tensor(
                out=z[:, h, t, :], in0=y_ps[t][:, a:b], scalar=gate[:, t : t + 1], in1=pull[k][:],
                op0=ALU.mult, op1=ALU.subtract,
            )

        z_grp = [grouped_tile(f"z_grp{h}", HALF) for h in range(2)]
        z_mx = [mx_tiles(f"z{h}", HALF) for h in range(2)]
        h_ps = [
            [ps.tile([P, HALF], F32, name=f"h_ps{h}_{t}", tag=f"bank{PACK * h + t}") for t in range(PACK)]
            for h in range(2)
        ]

        def places(h):
            codes, scales = z_mx[h]
            quantize(codes[:], scales[:], z_grp[h][:])
            for t in range(PACK):
                product(h_ps[h][t][:], w1w, w1s, t, codes[:], scales[:])

        def exp_rows(t, h):
            a, b = HALVES[h]
            nc.scalar.activation(out=ex[t][:, a:b], in_=h_ps[h][t][:], func=ACT.Exp, scale=0.5)

        for k in range(len(steps)):
            mix_gap(k)
            if k > 0:
                mix_out(k - 1)
            mix_pull(k)
            if k == PACK:
                group_on_vector(z_grp[0][:], z[:, 0])
            if k == PACK + 1:
                places(0)
        mix_out(len(steps) - 1)
        group_on_vector(z_grp[1][:], z[:, 1])
        places(1)
        for t in range(PACK):
            exp_rows(t, 0)

        out_rows = out_0.rearrange("(p t) j -> p t j", t=PACK)
        out_words = out_1[0].rearrange("p c r -> p (c r)").bitcast(I32)
        o_scales = sb.tile([P, H], U8, name="o_scales", align_bytes=64)
        res = [sb.tile([P, PACK, b - a], F32, name=f"res{c}") for c, (a, b) in enumerate(OUT_CHUNKS)]
        patches = [
            (c, t, first) for c, (a, b) in enumerate(OUT_CHUNKS) for t in range(PACK) for first in range(a, b, P)
        ]
        members, sums, recs, turned = {}, {}, {}, {}

        def patch_sums(k):
            c, t, first = patches[k]
            a, b = OUT_CHUNKS[c]
            if first == a:
                if c == 0:
                    exp_rows(t, 1)
                members[c, t] = sb.tile([P, (b - a) * MEMBERS], F32, name=f"mb{k}", tag="mb", bufs=3)
                fetch(members[c, t][:], ex[t], n3_l, a * MEMBERS, b * MEMBERS, scale=0.25, bias=0.03125)
            start = (first - a) * MEMBERS
            mb = members[c, t][:, start : start + P * MEMBERS].rearrange("p (j m) -> p j m", m=MEMBERS)
            sums[k] = ps.tile([P, P], F32, name=f"sums{k}", tag=f"bank{PACK + k % SUM_BANKS}")
            for m in range(MEMBERS):
                nc.tensor.matmul(
                    sums[k][:], lhsT=mb[:, :, m], rhs=ident[:], is_transpose=True,
                    start=(m == 0), stop=(m == MEMBERS - 1),
                )

        def patch_reciprocal(k):
            recs[k] = sb.tile([P, P], F32, name=f"rec{k}")
            nc.vector.reciprocal(out=recs[k][:], in_=sums[k][:])

        def patch_turn_back(k):
            turned[k] = ps.tile([P, P], F32, name=f"turned{k}", tag=f"bank{k % PACK}")
            nc.tensor.transpose(turned[k][:], recs[k][:], ident[:])

        def patch_result(k):
            c, t, first = patches[k]
            a, b = OUT_CHUNKS[c]
            nc.vector.tensor_tensor(
                out=res[c][:, t, first - a : first - a + P], in0=turned[k][:], in1=ex[t][:, first : first + P],
                op=ALU.mult,
            )
            if t == PACK - 1 and first + P == b:
                planes(c)

        def planes(c):
            a, b = OUT_CHUNKS[c]
            nc.sync.dma_start(out=out_rows[:, :, a:b], in_=res[c][:])
            o_grp = grouped_tile(f"o_grp{c}", b - a)
            group = group_on_vector if b == H else group_on_gpsimd
            group(o_grp[:], res[c][:])
            o_codes = sb.tile([P, b - a], U32, name=f"o_codes{c}", align_bytes=64)
            quantize(o_codes[:], o_scales[:, a:b], o_grp[:])
            nc.sync.dma_start(out=out_words[:, a:b], in_=o_codes[:].bitcast(I32))

        for k in range(len(patches)):
            patch_sums(k)
            if k > 0:
                patch_turn_back(k - 1)
            patch_reciprocal(k)
            if k > 0:
                patch_result(k - 1)
        patch_turn_back(len(patches) - 1)
        patch_result(len(patches) - 1)

        for q in range(4):
            nc.scalar.dma_start(
                out=out_2[0, 4 * q : 4 * q + 4, :].bitcast(I32), in_=o_scales[32 * q : 32 * q + 4, :].bitcast(I32)
            )
